import numpy as np
import ml_dtypes


def mxq(x, axis, fmt="e4m3"):
    dtype, down = {"e4m3": (ml_dtypes.float8_e4m3fn, 7), "e5m2": (ml_dtypes.float8_e5m2, 14)}[fmt]
    v = np.moveaxis(np.asarray(x, np.float32).astype(ml_dtypes.bfloat16).astype(np.float64), axis, -1)
    blocks = v.reshape(v.shape[:-1] + (-1, 32))
    amax = np.abs(blocks).max(-1, keepdims=True)
    byte = np.maximum(np.where(amax > 0, np.frexp(amax)[1] - 1 + 127, 0) - down, 1)
    scale = np.exp2(byte - 127.0)
    codes = (blocks / scale).astype(np.float32).astype(dtype).astype(np.float64)
    return np.moveaxis((codes * scale).reshape(v.shape), -1, axis)


WIDE = False


def mx_kscale(k):
    if not WIDE:
        return np.ones(k)
    levels = np.array([10, -10, 5, -5, 0])
    if k % 512:
        return np.exp2(np.random.permutation(np.resize(levels, k // 32))).repeat(32)
    a = np.empty((k // 512, 16))
    for p in range(k // 512):
        a[p, :8] = np.random.permutation(np.resize(levels, 8))
        for g in range(8):
            far = levels[np.abs(levels - a[p, g]) >= 10]
            a[p, g + 8] = far[np.random.randint(len(far))]
    return np.exp2(a.ravel()).repeat(32)


def f64(x):
    return np.asarray(x).astype(np.float64)


def striped(idx):
    return np.tile(idx.reshape(-1, 16).T, (8, 1)).astype(np.uint16)


def unstriped(offs):
    return offs[:16].T.reshape(-1).astype(np.int64)


E2M1 = np.array([0.0, 0.5, 1.0, 1.5, 2.0, 3.0, 4.0, 6.0, -0.0, -0.5, -1.0, -1.5, -2.0, -3.0, -4.0, -6.0])


def pack_weight(w, fmt):
    k, n = w.shape
    w = f64(np.asarray(w, np.float32).astype(ml_dtypes.bfloat16)).reshape(k // 32, 32, n)
    amax = np.abs(w).max(1)
    if fmt == "e4m3":
        byte = np.frexp(amax)[1] - 1 + 127 - 7
    else:
        mant, ex = np.frexp(amax / 6.0)
        byte = np.where(mant > 0.5, ex, ex - 1) + 127
    byte = np.clip(np.where(amax > 0, byte, 1), 1, 254)
    scaled = (w * np.exp2(127.0 - byte)[:, None, :]).reshape(k, n).astype(np.float32)
    by_word = np.ascontiguousarray(scaled.reshape(k // 512, 128, 4, n).transpose(0, 1, 3, 2))
    if fmt == "e4m3":
        words = by_word.astype(ml_dtypes.float8_e4m3fn).view(np.uint8)
    else:
        c = by_word.astype(ml_dtypes.float4_e2m1fn).view(np.uint8) & 0xF
        words = (c[..., 0::2] | (c[..., 1::2] << 4)).reshape(k // 512, 128, 2 * n)
    return np.ascontiguousarray(words), np.ascontiguousarray(byte.astype(np.uint8).reshape(k // 512, 16, n))


def unpack_weight(words, scales, fmt):
    g, _, n = scales.shape
    words = np.ascontiguousarray(words).reshape(g, 128, n, -1)
    if fmt == "e4m3":
        vals = words.view(ml_dtypes.float8_e4m3fn).astype(np.float64)
    else:
        nib = np.empty((g, 128, n, 4), np.uint8)
        nib[..., 0::2] = words & 0xF
        nib[..., 1::2] = words >> 4
        vals = E2M1[nib]
    vals = vals * np.repeat(np.exp2(scales.astype(np.float64) - 127.0), 8, axis=1)[..., None]
    return vals.transpose(0, 1, 3, 2).reshape(g * 512, n)


def gelu(v):
    return 0.5 * v * (1.0 + np.tanh(np.sqrt(2.0 / np.pi) * (v + 0.044715 * v**3)))


K, T, E, C, H, N = 512, 1024, 4, 128, 512, 512


def by_expert(wq, xq):
    return np.concatenate([wq[e].T @ xq[:, e * C:(e + 1) * C] for e in range(E)], axis=1)


def setup_inputs():
    n = np.random.standard_normal
    s = mx_kscale(K)
    u = mx_kscale(H)
    slot_token = np.random.permutation(T)[:E * C]
    x = pack_weight(n((K, T)) * s[:, None], "e4m3")
    w = [pack_weight(m, "e2m1") for m in n((E, K, N)) / np.sqrt(K) / s[None, :, None]]
    wa = [pack_weight(m, "e4m3") for m in n((E, K, H)) / np.sqrt(K) / s[None, :, None] * u]
    return {
        "x_words": x[0],
        "x_scales": x[1],
        "w_words": np.stack([m[0] for m in w]),
        "w_scales": np.stack([m[1] for m in w]),
        "wa_words": np.stack([m[0] for m in wa]),
        "wa_scales": np.stack([m[1] for m in wa]),
        "wb": (n((E, H, N)) / np.sqrt(H) / u[None, :, None]).astype(np.float32),
        "gate": np.tile(np.random.uniform(0.2, 1.0, E * C), (128, 1)).astype(np.float32),
        "offs": striped(slot_token),
    }


def reference(x_words, x_scales, w_words, w_scales, wa_words, wa_scales, wb, gate, offs):
    w = np.stack([unpack_weight(w_words[e], w_scales[e], "e2m1") for e in range(E)])
    wa = np.stack([unpack_weight(wa_words[e], wa_scales[e], "e4m3") for e in range(E)])
    wbq = mxq(f64(wb), 1, "e4m3")
    idx = unstriped(offs)
    xq = unpack_weight(x_words, x_scales, "e4m3")[:, idx]
    h = gelu(by_expert(wa, xq))
    y = by_expert(w, xq) + by_expert(wbq, mxq(h, 0, "e4m3"))
    out = np.zeros((N, T))
    out[:, idx] = f64(gate[:1]) * y
    return out

@@ -1,0 +1,221 @@
+from contextlib import ExitStack
+
+import concourse.mybir as mybir
+from concourse.masks import make_identity
+
+K, T, E, C, H, N = 512, 1024, 4, 128, 512, 512
+FLOPS = 2 * E * C * (K * H + K * N + H * N)
+
+F32 = mybir.dt.float32
+BF16 = mybir.dt.bfloat16
+I32 = mybir.dt.int32
+U32 = mybir.dt.uint32
+U16 = mybir.dt.uint16
+U8 = mybir.dt.uint8
+FP8X4 = mybir.dt.float8_e4m3fn_x4
+FP4X4 = mybir.dt.float4_e2m1fn_x4
+GELU = mybir.ActivationFunctionType.Gelu_apprx_tanh
+MULT = mybir.AluOpType.mult
+
+P = 128
+PACK = 4
+HALF = N // 2
+LIST_COLS = C // 16
+TAIL = 16
+
+
+def tile_moe_elr_gelu_kernel(
+    tc, x_words, x_scales, w_words, w_scales, wa_words, wa_scales, wb, gate, offs, out
+):
+    nc = tc.nc
+    with ExitStack() as ctx:
+        keep = ctx.enter_context(tc.tile_pool(name="keep", bufs=1))
+        ring = ctx.enter_context(tc.tile_pool(name="ring", bufs=3))
+        psum = ctx.enter_context(tc.psum_pool(name="psum", bufs=2))
+        psum_y = ctx.enter_context(tc.psum_pool(name="psum_y", bufs=4))
+
+        offsets = keep.tile([P, E * LIST_COLS], U16, name="offsets")
+        x_tab = keep.tile([P, T], U32, name="x_tab", align_bytes=64)
+        xs_tab = keep.tile([P, T], U8, name="xs_tab", align_bytes=64)
+        wa_plane = keep.tile([P, H], U8, name="wa_plane", align_bytes=64)
+        w_plane = keep.tile([P, E * N], U8, name="w_plane", align_bytes=64)
+        windows = [keep.tile([P, T], F32, name="window%d" % b) for b in range(N // P)]
+        ident = keep.tile([P, P], F32, name="ident")
+
+        nc.vector.memset(xs_tab[:].bitcast(I32), 0)
+        nc.vector.memset(wa_plane[:].bitcast(I32), 0)
+        nc.vector.memset(w_plane[:].bitcast(I32), 0)
+        for b in range(3):
+            nc.vector.memset(windows[b][:], 0.0)
+        nc.vector.memset(windows[3][:, : T - TAIL], 0.0)
+        nc.scalar.activation(windows[3][:, T - TAIL :], windows[0][:, :TAIL], GELU)
+        make_identity(nc, ident[:])
+
+        wa_sb, w_sb, gate_sb, wb_raw = {}, {}, {}, {}
+
+        def load_wa(e0, e1):
+            t = keep.tile([P, (e1 - e0) * H], U32, name="wa%d" % e0, align_bytes=64)
+            nc.sync.dma_start(
+                t[:].bitcast(I32).rearrange("p (e i) -> p e i", i=H),
+                wa_words[e0:e1, 0].rearrange("e p i d -> p e (i d)").bitcast(I32),
+            )
+            for e in range(e0, e1):
+                wa_sb[e] = t[:, (e - e0) * H : (e - e0 + 1) * H]
+
+        def load_w(e0, e1):
+            t = keep.tile([P, (e1 - e0) * 2 * N], U8, name="w%d" % e0, align_bytes=64)
+            nc.sync.dma_start(
+                t[:].bitcast(I32).rearrange("p (e n) -> p e n", e=e1 - e0),
+                w_words[e0:e1, 0].rearrange("e p n -> p e n").bitcast(I32),
+            )
+            for e in range(e0, e1):
+                w_sb[e] = t[:, (e - e0) * 2 * N : (e - e0 + 1) * 2 * N]
+
+        def load_gate(e0, e1):
+            t = keep.tile([P, (e1 - e0) * C], F32, name="gate%d" % e0)
+            nc.sync.dma_start(t[:], gate[:, e0 * C : e1 * C])
+            gate_sb[e0] = t
+
+        def load_wb(e, h):
+            t = keep.tile([P, PACK, HALF], F32, name="wb%d_%d" % (e, h))
+            nc.sync.dma_start(t[:], wb[e, :, h * HALF : (h + 1) * HALF].rearrange("(p j) n -> p j n", j=PACK))
+            wb_raw[e, h] = t
+
+        nc.sync.dma_start(offsets[:], offs)
+        nc.sync.dma_start(x_tab[:].bitcast(I32), x_words[0].rearrange("p t d -> p (t d)").bitcast(I32))
+        for r in range(4):
+            nc.sync.dma_start(xs_tab[r:P:32, :].bitcast(I32), x_scales[0, r:16:4, :].bitcast(I32))
+        load_wa(0, 1)
+        for q in range(4):
+            nc.sync.dma_start(
+                wa_plane[32 * q : 32 * q + 16, :].bitcast(I32), wa_scales[:, 0, 4 * q : 4 * q + 4, :].bitcast(I32)
+            )
+        load_wb(0, 0)
+        load_w(0, 1)
+        for r in range(4):
+            nc.sync.dma_start(
+                w_plane[r:P:32, :].bitcast(I32).rearrange("q (e n) -> q e n", e=E),
+                w_scales[:, 0, r:16:4, :].rearrange("e q n -> q e n").bitcast(I32),
+            )
+        load_gate(0, 2)
+        load_wb(0, 1)
+        load_wa(1, 2)
+        load_w(1, 4)
+        load_wb(1, 0)
+        load_wb(1, 1)
+        load_wa(2, 4)
+        load_gate(2, 4)
+        load_wb(2, 0)
+        load_wb(3, 0)
+        load_wb(2, 1)
+        load_wb(3, 1)
+
+        xg, xgs, hq, hqs, wbq, wbqs = {}, {}, {}, {}, {}, {}
+        y_sb = [keep.tile([P, 2, E * C], F32, name="y%d" % h) for h in range(2)]
+
+        def gather(e0, e1):
+            lst = offsets[:, e0 * LIST_COLS : e1 * LIST_COLS]
+            words = keep.tile([P, (e1 - e0) * C], U32, name="xg%d" % e0, align_bytes=64)
+            scales = keep.tile([P, (e1 - e0) * C], U8, name="xgs%d" % e0, align_bytes=64)
+            nc.vector.tensor_copy(words[:], x_tab[:].indirect(lst))
+            nc.vector.tensor_copy(scales[:], xs_tab[:].indirect(lst))
+            for e in range(e0, e1):
+                xg[e] = words[:, (e - e0) * C : (e - e0 + 1) * C].bitcast(FP8X4)
+                xgs[e] = scales[:, (e - e0) * C : (e - e0 + 1) * C]
+
+        def hidden(e):
+            pre = psum.tile([P, H], F32, name="pre")
+            nc.tensor.matmul_mx(
+                out=pre[:], lhsT=xg[e], lhsT_scale=xgs[e], rhs=wa_sb[e].bitcast(FP8X4),
+                rhs_scale=wa_plane[4 * e :, :], start=True, stop=True,
+            )
+            act = ring.tile([P, H], BF16, name="act", align_bytes=64)
+            nc.scalar.activation(
+                act[:].rearrange("s (u p d) -> s u p d", u=2, d=2),
+                pre[:].rearrange("s (p u d) -> s u p d", u=2, d=2),
+                GELU,
+            )
+            turned = psum.tile([P, 2, C], F32, name="turned")
+            pairs = act[:].bitcast(F32)
+            for u in range(2):
+                nc.tensor.transpose(turned[:, u, :], pairs[:, u * P : (u + 1) * P], ident[:])
+            grouped = ring.tile([P, C * PACK], BF16, name="h_grouped", align_bytes=64)
+            nc.scalar.copy(
+                grouped[:].bitcast(F32).rearrange("p (s u) -> p s u", u=2), turned[:].rearrange("p u s -> p s u")
+            )
+            codes = keep.tile([P, C], U32, name="hq%d" % e, align_bytes=64)
+            scales = keep.tile([P, C], U8, name="hqs%d" % e, align_bytes=64)
+            nc.vector.quantize_mx(out=codes[:].bitcast(FP8X4), scales=scales[:], in_=grouped[:])
+            hq[e], hqs[e] = codes, scales
+
+        def quantize_wb(e, h, copy):
+            grouped = ring.tile([P, HALF * PACK], BF16, name="wb_grouped", align_bytes=64)
+            copy(
+                grouped[:].rearrange("p (c i t) -> p c t i", i=4, t=PACK),
+                wb_raw[e, h][:].rearrange("p t (c i) -> p c t i", i=4),
+            )
+            codes = keep.tile([P, HALF], U32, name="wbq%d_%d" % (e, h), align_bytes=64)
+            scales = keep.tile([P, HALF], U8, name="wbqs%d_%d" % (e, h), align_bytes=64)
+            nc.vector.quantize_mx(out=codes[:].bitcast(FP8X4), scales=scales[:], in_=grouped[:])
+            wbq[e, h], wbqs[e, h] = codes, scales
+
+        def product(e, h):
+            acc = psum_y.tile([P, 2, C], F32, name="acc")
+            for b in range(2):
+                n0 = h * HALF + b * P
+                nc.tensor.matmul_mx(
+                    out=acc[:, b, :], lhsT=w_sb[e][:, 2 * n0 : 2 * (n0 + P)].bitcast(FP4X4),
+                    lhsT_scale=w_plane[:, e * N + n0 : e * N + n0 + P], rhs=xg[e], rhs_scale=xgs[e],
+                    start=True, stop=False,
+                )
+                nc.tensor.matmul_mx(
+                    out=acc[:, b, :], lhsT=wbq[e, h][:, b * P : (b + 1) * P].bitcast(FP8X4),
+                    lhsT_scale=wbqs[e, h][:, b * P : (b + 1) * P], rhs=hq[e][:].bitcast(FP8X4),
+                    rhs_scale=hqs[e][:], start=False, stop=True,
+                )
+            nc.scalar.copy(y_sb[h][:, :, e * C : (e + 1) * C], acc[:])
+
+        def scatter(e0, e1, h, store):
+            g0 = e0 - e0 % 2
+            for b in range(2):
+                window = windows[2 * h + b]
+                nc.vector.tensor_tensor(
+                    window[:].indirect(offsets[:, e0 * LIST_COLS : e1 * LIST_COLS]),
+                    y_sb[h][:, b, e0 * C : e1 * C],
+                    gate_sb[g0][:, (e0 - g0) * C : (e1 - g0) * C],
+                    MULT,
+                )
+                if store:
+                    n0 = h * HALF + b * P
+                    nc.sync.dma_start(out[n0 : n0 + P, :], window[:])
+
+        gather(0, 1)
+        hidden(0)
+        gather(1, 2)
+        gather(2, 4)
+        quantize_wb(0, 0, nc.vector.tensor_copy)
+        product(0, 0)
+        quantize_wb(0, 1, nc.scalar.copy)
+        scatter(0, 1, 0, False)
+        hidden(1)
+        product(0, 1)
+        quantize_wb(1, 0, nc.scalar.copy)
+        scatter(0, 1, 1, False)
+        product(1, 0)
+        quantize_wb(1, 1, nc.scalar.copy)
+        scatter(1, 2, 0, False)
+        hidden(2)
+        product(1, 1)
+        quantize_wb(2, 0, nc.scalar.copy)
+        scatter(1, 2, 1, False)
+        hidden(3)
+        product(2, 0)
+        quantize_wb(3, 0, nc.scalar.copy)
+        scatter(2, 3, 0, False)
+        product(3, 0)
+        quantize_wb(2, 1, nc.scalar.copy)
+        product(2, 1)
+        quantize_wb(3, 1, nc.scalar.copy)
+        scatter(3, 4, 0, True)
+        product(3, 1)
+        scatter(2, 4, 1, True)

@@ -21,7 +21,6 @@ P = 128
 PACK = 4
 HALF = N // 2
 LIST_COLS = C // 16
-TAIL = 16
 
 
 def tile_moe_elr_gelu_kernel(
@@ -42,13 +41,14 @@ def tile_moe_elr_gelu_kernel(
         windows = [keep.tile([P, T], F32, name="window%d" % b) for b in range(N // P)]
         ident = keep.tile([P, P], F32, name="ident")
 
-        nc.vector.memset(xs_tab[:].bitcast(I32), 0)
+        zero = keep.tile([P, 8], F32, name="zero")
         nc.vector.memset(wa_plane[:].bitcast(I32), 0)
+        nc.vector.memset(zero[:], 0.0)
         nc.vector.memset(w_plane[:].bitcast(I32), 0)
-        for b in range(3):
+        for b in range(2):
             nc.vector.memset(windows[b][:], 0.0)
-        nc.vector.memset(windows[3][:, : T - TAIL], 0.0)
-        nc.scalar.activation(windows[3][:, T - TAIL :], windows[0][:, :TAIL], GELU)
+        for b in range(2, 4):
+            nc.scalar.activation(windows[b][:], zero[:, 0:1].to_broadcast([P, T]), GELU)
         make_identity(nc, ident[:])
 
         wa_sb, w_sb, gate_sb, wb_raw = {}, {}, {}, {}
@@ -77,15 +77,18 @@ def tile_moe_elr_gelu_kernel(
             gate_sb[e0] = t
 
         def load_wb(e, h):
-            t = keep.tile([P, PACK, HALF], F32, name="wb%d_%d" % (e, h))
-            nc.sync.dma_start(t[:], wb[e, :, h * HALF : (h + 1) * HALF].rearrange("(p j) n -> p j n", j=PACK))
+            t = keep.tile([P, PACK * HALF], F32, name="wb%d_%d" % (e, h), align_bytes=64)
+            nc.sync.dma_start(t[:].rearrange("p (j n) -> p j n", j=PACK), wb[e, :, h * HALF : (h + 1) * HALF].rearrange("(p j) n -> p j n", j=PACK))
             wb_raw[e, h] = t
 
         nc.sync.dma_start(offsets[:], offs)
+        for q in range(4):
+            rows = x_scales[0, 4 * q : 4 * q + 4, :].bitcast(I32)
+            nc.sync.dma_start(
+                xs_tab[32 * q : 32 * q + 32, :].bitcast(I32), rows.unsqueeze(0).to_broadcast([8, 4, T // 4])
+            )
         nc.sync.dma_start(x_tab[:].bitcast(I32), x_words[0].rearrange("p t d -> p (t d)").bitcast(I32))
-        for r in range(4):
-            nc.sync.dma_start(xs_tab[r:P:32, :].bitcast(I32), x_scales[0, r:16:4, :].bitcast(I32))
-        load_wa(0, 1)
+        load_wa(0, 2)
         for q in range(4):
             nc.sync.dma_start(
                 wa_plane[32 * q : 32 * q + 16, :].bitcast(I32), wa_scales[:, 0, 4 * q : 4 * q + 4, :].bitcast(I32)
@@ -99,19 +102,20 @@ def tile_moe_elr_gelu_kernel(
             )
         load_gate(0, 2)
         load_wb(0, 1)
-        load_wa(1, 2)
-        load_w(1, 4)
+        load_w(1, 2)
         load_wb(1, 0)
+        load_wa(2, 3)
         load_wb(1, 1)
-        load_wa(2, 4)
-        load_gate(2, 4)
+        load_wa(3, 4)
         load_wb(2, 0)
+        load_w(2, 4)
+        load_gate(2, 4)
         load_wb(3, 0)
         load_wb(2, 1)
         load_wb(3, 1)
 
         xg, xgs, hq, hqs, wbq, wbqs = {}, {}, {}, {}, {}, {}
-        y_sb = [keep.tile([P, 2, E * C], F32, name="y%d" % h) for h in range(2)]
+        y_sb, turned_ps = {}, {}
 
         def gather(e0, e1):
             lst = offsets[:, e0 * LIST_COLS : e1 * LIST_COLS]
@@ -139,27 +143,27 @@ def tile_moe_elr_gelu_kernel(
             pairs = act[:].bitcast(F32)
             for u in range(2):
                 nc.tensor.transpose(turned[:, u, :], pairs[:, u * P : (u + 1) * P], ident[:])
-            grouped = ring.tile([P, C * PACK], BF16, name="h_grouped", align_bytes=64)
-            nc.scalar.copy(
-                grouped[:].bitcast(F32).rearrange("p (s u) -> p s u", u=2), turned[:].rearrange("p u s -> p s u")
-            )
+            turned_ps[e] = turned
+
+        def quantize_hidden(e, words):
+            nc.scalar.copy(words.rearrange("p (s u) -> p s u", u=2), turned_ps[e][:].rearrange("p u s -> p s u"))
             codes = keep.tile([P, C], U32, name="hq%d" % e, align_bytes=64)
             scales = keep.tile([P, C], U8, name="hqs%d" % e, align_bytes=64)
-            nc.vector.quantize_mx(out=codes[:].bitcast(FP8X4), scales=scales[:], in_=grouped[:])
+            nc.vector.quantize_mx(out=codes[:].bitcast(FP8X4), scales=scales[:], in_=words.bitcast(BF16))
             hq[e], hqs[e] = codes, scales
 
         def quantize_wb(e, h, copy):
             grouped = ring.tile([P, HALF * PACK], BF16, name="wb_grouped", align_bytes=64)
             copy(
                 grouped[:].rearrange("p (c i t) -> p c t i", i=4, t=PACK),
-                wb_raw[e, h][:].rearrange("p t (c i) -> p c t i", i=4),
+                wb_raw[e, h][:].rearrange("p (t c i) -> p c t i", t=PACK, i=4),
             )
             codes = keep.tile([P, HALF], U32, name="wbq%d_%d" % (e, h), align_bytes=64)
             scales = keep.tile([P, HALF], U8, name="wbqs%d_%d" % (e, h), align_bytes=64)
             nc.vector.quantize_mx(out=codes[:].bitcast(FP8X4), scales=scales[:], in_=grouped[:])
             wbq[e, h], wbqs[e, h] = codes, scales
 
-        def product(e, h):
+        def product(e, h, home, col0):
             acc = psum_y.tile([P, 2, C], F32, name="acc")
             for b in range(2):
                 n0 = h * HALF + b * P
@@ -173,7 +177,9 @@ def tile_moe_elr_gelu_kernel(
                     lhsT_scale=wbqs[e, h][:, b * P : (b + 1) * P], rhs=hq[e][:].bitcast(FP8X4),
                     rhs_scale=hqs[e][:], start=False, stop=True,
                 )
-            nc.scalar.copy(y_sb[h][:, :, e * C : (e + 1) * C], acc[:])
+            rows = home.rearrange("p (b s) -> p b s", b=2)
+            nc.scalar.copy(rows[:, :, col0 : col0 + C], acc[:])
+            y_sb[e, h] = rows
 
         def scatter(e0, e1, h, store):
             g0 = e0 - e0 % 2
@@ -181,7 +187,7 @@ def tile_moe_elr_gelu_kernel(
                 window = windows[2 * h + b]
                 nc.vector.tensor_tensor(
                     window[:].indirect(offsets[:, e0 * LIST_COLS : e1 * LIST_COLS]),
-                    y_sb[h][:, b, e0 * C : e1 * C],
+                    y_sb[e0, h][:, b, :],
                     gate_sb[g0][:, (e0 - g0) * C : (e1 - g0) * C],
                     MULT,
                 )
@@ -189,33 +195,40 @@ def tile_moe_elr_gelu_kernel(
                     n0 = h * HALF + b * P
                     nc.sync.dma_start(out[n0 : n0 + P, :], window[:])
 
+        def fresh(name):
+            return keep.tile([P, 2 * C], F32, name=name, align_bytes=64)[:]
+
         gather(0, 1)
         hidden(0)
         gather(1, 2)
+        hidden(1)
         gather(2, 4)
         quantize_wb(0, 0, nc.vector.tensor_copy)
-        product(0, 0)
-        quantize_wb(0, 1, nc.scalar.copy)
+        quantize_hidden(0, fresh("h0"))
+        product(0, 0, fresh("y00"), 0)
+        quantize_hidden(1, fresh("h1"))
         scatter(0, 1, 0, False)
-        hidden(1)
-        product(0, 1)
-        quantize_wb(1, 0, nc.scalar.copy)
+        quantize_wb(0, 1, nc.scalar.copy)
+        quantize_wb(1, 0, nc.vector.tensor_copy)
+        product(0, 1, fresh("y01"), 0)
         scatter(0, 1, 1, False)
-        product(1, 0)
-        quantize_wb(1, 1, nc.scalar.copy)
-        scatter(1, 2, 0, False)
         hidden(2)
-        product(1, 1)
-        quantize_wb(2, 0, nc.scalar.copy)
-        scatter(1, 2, 1, False)
+        quantize_hidden(2, fresh("h2"))
+        quantize_wb(1, 1, nc.scalar.copy)
+        product(1, 0, wb_raw[1, 1][:, : 2 * C], 0)
+        scatter(1, 2, 0, False)
         hidden(3)
-        product(2, 0)
+        quantize_wb(2, 0, nc.scalar.copy)
+        product(1, 1, wb_raw[2, 0][:, : 2 * C], 0)
+        scatter(1, 2, 1, False)
+        quantize_hidden(3, wb_raw[2, 0][:, 2 * C : 4 * C])
         quantize_wb(3, 0, nc.scalar.copy)
+        product(2, 0, wb_raw[3, 0][:, : 2 * C], 0)
         scatter(2, 3, 0, False)
-        product(3, 0)
         quantize_wb(2, 1, nc.scalar.copy)
-        product(2, 1)
         quantize_wb(3, 1, nc.scalar.copy)
+        product(3, 0, wb_raw[3, 1][:, : 2 * C], 0)
         scatter(3, 4, 0, True)
-        product(3, 1)
+        product(2, 1, wb_raw[3, 1][:, 4 * C :], 0)
+        product(3, 1, wb_raw[3, 1][:, 4 * C :], C)
         scatter(2, 4, 1, True)

@@ -76,10 +76,12 @@ def tile_moe_elr_gelu_kernel(
             nc.sync.dma_start(t[:], gate[:, e0 * C : e1 * C])
             gate_sb[e0] = t
 
-        def load_wb(e, h):
-            t = keep.tile([P, PACK * HALF], F32, name="wb%d_%d" % (e, h), align_bytes=64)
-            nc.sync.dma_start(t[:].rearrange("p (j n) -> p j n", j=PACK), wb[e, :, h * HALF : (h + 1) * HALF].rearrange("(p j) n -> p j n", j=PACK))
-            wb_raw[e, h] = t
+        def load_wb(e, h0, h1):
+            t = keep.tile([P, PACK * (h1 - h0) * HALF], F32, name="wb%d_%d" % (e, h0), align_bytes=64)
+            rows = t[:].rearrange("p (j n) -> p j n", j=PACK)
+            nc.sync.dma_start(rows, wb[e, :, h0 * HALF : h1 * HALF].rearrange("(p j) n -> p j n", j=PACK))
+            for h in range(h0, h1):
+                wb_raw[e, h] = rows[:, :, (h - h0) * HALF : (h - h0 + 1) * HALF]
 
         nc.sync.dma_start(offsets[:], offs)
         for q in range(4):
@@ -93,29 +95,24 @@ def tile_moe_elr_gelu_kernel(
             nc.sync.dma_start(
                 wa_plane[32 * q : 32 * q + 16, :].bitcast(I32), wa_scales[:, 0, 4 * q : 4 * q + 4, :].bitcast(I32)
             )
-        load_wb(0, 0)
-        load_w(0, 1)
+        load_wb(0, 0, 1)
+        load_wb(0, 1, 2)
+        load_w(0, 2)
+        load_gate(0, 2)
         for r in range(4):
             nc.sync.dma_start(
                 w_plane[r:P:32, :].bitcast(I32).rearrange("q (e n) -> q e n", e=E),
                 w_scales[:, 0, r:16:4, :].rearrange("e q n -> q e n").bitcast(I32),
             )
-        load_gate(0, 2)
-        load_wb(0, 1)
-        load_w(1, 2)
-        load_wb(1, 0)
-        load_wa(2, 3)
-        load_wb(1, 1)
-        load_wa(3, 4)
-        load_wb(2, 0)
+        load_wb(1, 0, 2)
+        load_wa(2, 4)
+        load_wb(2, 0, 2)
         load_w(2, 4)
         load_gate(2, 4)
-        load_wb(3, 0)
-        load_wb(2, 1)
-        load_wb(3, 1)
+        load_wb(3, 0, 2)
 
         xg, xgs, hq, hqs, wbq, wbqs = {}, {}, {}, {}, {}, {}
-        y_sb, turned_ps = {}, {}
+        turned_ps = {}
 
         def gather(e0, e1):
             lst = offsets[:, e0 * LIST_COLS : e1 * LIST_COLS]
@@ -156,47 +153,54 @@ def tile_moe_elr_gelu_kernel(
             grouped = ring.tile([P, HALF * PACK], BF16, name="wb_grouped", align_bytes=64)
             copy(
                 grouped[:].rearrange("p (c i t) -> p c t i", i=4, t=PACK),
-                wb_raw[e, h][:].rearrange("p (t c i) -> p c t i", t=PACK, i=4),
+                wb_raw[e, h].rearrange("p t (c i) -> p c t i", i=4),
             )
             codes = keep.tile([P, HALF], U32, name="wbq%d_%d" % (e, h), align_bytes=64)
             scales = keep.tile([P, HALF], U8, name="wbqs%d_%d" % (e, h), align_bytes=64)
             nc.vector.quantize_mx(out=codes[:].bitcast(FP8X4), scales=scales[:], in_=grouped[:])
             wbq[e, h], wbqs[e, h] = codes, scales
 
-        def product(e, h, home, col0):
-            acc = psum_y.tile([P, 2, C], F32, name="acc")
-            for b in range(2):
-                n0 = h * HALF + b * P
+        def product(e, blocks, home):
+            acc = psum_y.tile([P, len(blocks), C], F32, name="acc")
+            for a, b in enumerate(blocks):
+                h, m0, n0 = b // 2, (b % 2) * P, b * P
                 nc.tensor.matmul_mx(
-                    out=acc[:, b, :], lhsT=w_sb[e][:, 2 * n0 : 2 * (n0 + P)].bitcast(FP4X4),
+                    out=acc[:, a, :], lhsT=w_sb[e][:, 2 * n0 : 2 * (n0 + P)].bitcast(FP4X4),
                     lhsT_scale=w_plane[:, e * N + n0 : e * N + n0 + P], rhs=xg[e], rhs_scale=xgs[e],
                     start=True, stop=False,
                 )
                 nc.tensor.matmul_mx(
-                    out=acc[:, b, :], lhsT=wbq[e, h][:, b * P : (b + 1) * P].bitcast(FP8X4),
-                    lhsT_scale=wbqs[e, h][:, b * P : (b + 1) * P], rhs=hq[e][:].bitcast(FP8X4),
+                    out=acc[:, a, :], lhsT=wbq[e, h][:, m0 : m0 + P].bitcast(FP8X4),
+                    lhsT_scale=wbqs[e, h][:, m0 : m0 + P], rhs=hq[e][:].bitcast(FP8X4),
                     rhs_scale=hqs[e][:], start=False, stop=True,
                 )
-            rows = home.rearrange("p (b s) -> p b s", b=2)
-            nc.scalar.copy(rows[:, :, col0 : col0 + C], acc[:])
-            y_sb[e, h] = rows
+            nc.scalar.copy(home, acc[:])
 
-        def scatter(e0, e1, h, store):
+        def scatter(e0, e1, b, values, store):
             g0 = e0 - e0 % 2
-            for b in range(2):
-                window = windows[2 * h + b]
-                nc.vector.tensor_tensor(
-                    window[:].indirect(offsets[:, e0 * LIST_COLS : e1 * LIST_COLS]),
-                    y_sb[e0, h][:, b, :],
-                    gate_sb[g0][:, (e0 - g0) * C : (e1 - g0) * C],
-                    MULT,
-                )
-                if store:
-                    n0 = h * HALF + b * P
-                    nc.sync.dma_start(out[n0 : n0 + P, :], window[:])
+            nc.vector.tensor_tensor(
+                windows[b][:].indirect(offsets[:, e0 * LIST_COLS : e1 * LIST_COLS]),
+                values,
+                gate_sb[g0][:, (e0 - g0) * C : (e1 - g0) * C],
+                MULT,
+            )
+            if store:
+                nc.sync.dma_start(out[b * P : (b + 1) * P, :], windows[b][:])
 
-        def fresh(name):
-            return keep.tile([P, 2 * C], F32, name=name, align_bytes=64)[:]
+        def fresh(name, blocks):
+            return keep.tile([P, blocks, C], F32, name=name, align_bytes=64)[:]
+
+        def unit(e, h, home, store):
+            product(e, [2 * h, 2 * h + 1], home)
+            for a in range(2):
+                scatter(e, e + 1, 2 * h + a, home[:, a, :], store)
+
+        def single(e, b, home):
+            product(e, [b], home)
+            scatter(e, e + 1, b, home[:, 0, :], False)
+
+        def spent(e, h, j):
+            return wb_raw[e, h][:, j, :].rearrange("p (a s) -> p a s", a=2)
 
         gather(0, 1)
         hidden(0)
@@ -204,31 +208,29 @@ def tile_moe_elr_gelu_kernel(
         hidden(1)
         gather(2, 4)
         quantize_wb(0, 0, nc.vector.tensor_copy)
-        quantize_hidden(0, fresh("h0"))
-        product(0, 0, fresh("y00"), 0)
-        quantize_hidden(1, fresh("h1"))
-        scatter(0, 1, 0, False)
-        quantize_wb(0, 1, nc.scalar.copy)
-        quantize_wb(1, 0, nc.vector.tensor_copy)
-        product(0, 1, fresh("y01"), 0)
-        scatter(0, 1, 1, False)
-        hidden(2)
-        quantize_hidden(2, fresh("h2"))
+        quantize_hidden(0, fresh("h0", 2).rearrange("p a s -> p (a s)"))
+        single(0, 0, fresh("y0", 1))
+        single(0, 1, fresh("y1", 1))
+        quantize_wb(0, 1, nc.vector.tensor_copy)
+        quantize_hidden(1, fresh("h1", 2).rearrange("p a s -> p (a s)"))
+        single(0, 2, fresh("y2", 1))
+        quantize_wb(1, 0, nc.scalar.copy)
+        single(0, 3, spent(1, 0, 0)[:, 0:1, :])
         quantize_wb(1, 1, nc.scalar.copy)
-        product(1, 0, wb_raw[1, 1][:, : 2 * C], 0)
-        scatter(1, 2, 0, False)
-        hidden(3)
+        unit(1, 0, spent(1, 1, 0), False)
+        hidden(2)
+        quantize_hidden(2, fresh("h2", 2).rearrange("p a s -> p (a s)"))
         quantize_wb(2, 0, nc.scalar.copy)
-        product(1, 1, wb_raw[2, 0][:, : 2 * C], 0)
-        scatter(1, 2, 1, False)
-        quantize_hidden(3, wb_raw[2, 0][:, 2 * C : 4 * C])
+        unit(1, 1, spent(2, 0, 0), False)
+        hidden(3)
         quantize_wb(3, 0, nc.scalar.copy)
-        product(2, 0, wb_raw[3, 0][:, : 2 * C], 0)
-        scatter(2, 3, 0, False)
+        quantize_hidden(3, wb_raw[3, 0][:, 1, :])
+        unit(2, 0, spent(3, 0, 0), False)
         quantize_wb(2, 1, nc.scalar.copy)
         quantize_wb(3, 1, nc.scalar.copy)
-        product(3, 0, wb_raw[3, 1][:, : 2 * C], 0)
-        scatter(3, 4, 0, True)
-        product(2, 1, wb_raw[3, 1][:, 4 * C :], 0)
-        product(3, 1, wb_raw[3, 1][:, 4 * C :], C)
-        scatter(2, 4, 1, True)
+        unit(3, 0, spent(3, 1, 0), True)
+        last = wb_raw[3, 1][:, 1:3, :]
+        product(2, [2, 3], last[:, :, :C])
+        product(3, [2, 3], last[:, :, C:])
+        for a in range(2):
+            scatter(2, 4, 2 + a, last[:, a, :], True)

@@ -29,9 +29,7 @@ def tile_moe_elr_gelu_kernel(
     nc = tc.nc
     with ExitStack() as ctx:
         keep = ctx.enter_context(tc.tile_pool(name="keep", bufs=1))
-        ring = ctx.enter_context(tc.tile_pool(name="ring", bufs=3))
-        psum = ctx.enter_context(tc.psum_pool(name="psum", bufs=2))
-        psum_y = ctx.enter_context(tc.psum_pool(name="psum_y", bufs=4))
+        psum = ctx.enter_context(tc.psum_pool(name="psum", bufs=1))
 
         offsets = keep.tile([P, E * LIST_COLS], U16, name="offsets")
         x_tab = keep.tile([P, T], U32, name="x_tab", align_bytes=64)
@@ -40,6 +38,22 @@ def tile_moe_elr_gelu_kernel(
         w_plane = keep.tile([P, E * N], U8, name="w_plane", align_bytes=64)
         windows = [keep.tile([P, T], F32, name="window%d" % b) for b in range(N // P)]
         ident = keep.tile([P, P], F32, name="ident")
+        wb_flat = {
+            (g, h): keep.tile([P, P + 2 * PACK * HALF], F32, name="wb%d_%d" % (g, h), align_bytes=64)
+            for g in range(2)
+            for h in range(2)
+            if (g, h) == (1, 1)
+        }
+        wb_raw = {key: t[:, P:].rearrange("p (e j n) -> p e j n", e=2, j=PACK) for key, t in wb_flat.items()}
+        wb_own = {
+            (e, h): keep.tile([P, PACK, HALF], F32, name="own%d_%d" % (e, h), tag="own%d_%d" % (e, h), align_bytes=64)
+            for e in range(E)
+            for h in range(2)
+            if e < 2 or h == 0
+        }
+
+        def raw_half(e, h):
+            return wb_own[e, h][:] if (e, h) in wb_own else wb_raw[e // 2, h][:, e % 2]
 
         zero = keep.tile([P, 8], F32, name="zero")
         nc.vector.memset(wa_plane[:].bitcast(I32), 0)
@@ -51,7 +65,27 @@ def tile_moe_elr_gelu_kernel(
             nc.scalar.activation(windows[b][:], zero[:, 0:1].to_broadcast([P, T]), GELU)
         make_identity(nc, ident[:])
 
-        wa_sb, w_sb, gate_sb, wb_raw = {}, {}, {}, {}
+        wa_sb, w_sb, gate_sb = {}, {}, {}
+
+        def load_x():
+            nc.sync.dma_start(x_tab[:].bitcast(I32), x_words[0].rearrange("p t d -> p (t d)").bitcast(I32))
+
+        def load_x_scales(q):
+            rows = x_scales[0, 4 * q : 4 * q + 4, :].bitcast(I32)
+            nc.sync.dma_start(
+                xs_tab[32 * q : 32 * q + 32, :].bitcast(I32), rows.unsqueeze(0).to_broadcast([8, 4, T // 4])
+            )
+
+        def load_wa_scales(q, queue):
+            queue.dma_start(
+                wa_plane[32 * q : 32 * q + 16, :].bitcast(I32), wa_scales[:, 0, 4 * q : 4 * q + 4, :].bitcast(I32)
+            )
+
+        def load_w_scales(r, queue):
+            queue.dma_start(
+                w_plane[r:P:32, :].bitcast(I32).rearrange("q (e n) -> q e n", e=E),
+                w_scales[:, 0, r:16:4, :].rearrange("e q n -> q e n").bitcast(I32),
+            )
 
         def load_wa(e0, e1):
             t = keep.tile([P, (e1 - e0) * H], U32, name="wa%d" % e0, align_bytes=64)
@@ -74,45 +108,40 @@ def tile_moe_elr_gelu_kernel(
         def load_gate(e0, e1):
             t = keep.tile([P, (e1 - e0) * C], F32, name="gate%d" % e0)
             nc.sync.dma_start(t[:], gate[:, e0 * C : e1 * C])
-            gate_sb[e0] = t
+            for e in range(e0, e1):
+                gate_sb[e] = (t, (e - e0) * C)
 
-        def load_wb(e, h0, h1):
-            t = keep.tile([P, PACK * (h1 - h0) * HALF], F32, name="wb%d_%d" % (e, h0), align_bytes=64)
-            rows = t[:].rearrange("p (j n) -> p j n", j=PACK)
-            nc.sync.dma_start(rows, wb[e, :, h0 * HALF : h1 * HALF].rearrange("(p j) n -> p j n", j=PACK))
-            for h in range(h0, h1):
-                wb_raw[e, h] = rows[:, :, (h - h0) * HALF : (h - h0 + 1) * HALF]
+        def load_wb(e, h):
+            nc.sync.dma_start(
+                raw_half(e, h), wb[e, :, h * HALF : (h + 1) * HALF].rearrange("(p j) n -> p j n", j=PACK)
+            )
 
         nc.sync.dma_start(offsets[:], offs)
         for q in range(4):
-            rows = x_scales[0, 4 * q : 4 * q + 4, :].bitcast(I32)
-            nc.sync.dma_start(
-                xs_tab[32 * q : 32 * q + 32, :].bitcast(I32), rows.unsqueeze(0).to_broadcast([8, 4, T // 4])
-            )
-        nc.sync.dma_start(x_tab[:].bitcast(I32), x_words[0].rearrange("p t d -> p (t d)").bitcast(I32))
-        load_wa(0, 2)
+            load_x_scales(q)
+        load_x()
+        load_wa(0, 1)
         for q in range(4):
-            nc.sync.dma_start(
-                wa_plane[32 * q : 32 * q + 16, :].bitcast(I32), wa_scales[:, 0, 4 * q : 4 * q + 4, :].bitcast(I32)
-            )
-        load_wb(0, 0, 1)
-        load_wb(0, 1, 2)
+            load_wa_scales(q, nc.sync)
+        load_wa(1, 2)
+        load_wb(0, 0)
+        load_wb(0, 1)
         load_w(0, 2)
-        load_gate(0, 2)
         for r in range(4):
-            nc.sync.dma_start(
-                w_plane[r:P:32, :].bitcast(I32).rearrange("q (e n) -> q e n", e=E),
-                w_scales[:, 0, r:16:4, :].rearrange("e q n -> q e n").bitcast(I32),
-            )
-        load_wb(1, 0, 2)
-        load_wa(2, 4)
-        load_wb(2, 0, 2)
+            load_w_scales(r, nc.sync)
+        load_wb(1, 0)
+        load_gate(0, 2)
+        load_wb(1, 1)
+        load_wa(2, 3)
+        load_wb(2, 0)
+        load_wa(3, 4)
+        load_wb(3, 0)
         load_w(2, 4)
+        load_wb(2, 1)
+        load_wb(3, 1)
         load_gate(2, 4)
-        load_wb(3, 0, 2)
 
-        xg, xgs, hq, hqs, wbq, wbqs = {}, {}, {}, {}, {}, {}
-        turned_ps = {}
+        xg, xgs, act, turned, hq, hqs, grouped, wbq, wbqs = {}, {}, {}, {}, {}, {}, {}, {}, {}
 
         def gather(e0, e1):
             lst = offsets[:, e0 * LIST_COLS : e1 * LIST_COLS]
@@ -124,113 +153,177 @@ def tile_moe_elr_gelu_kernel(
                 xg[e] = words[:, (e - e0) * C : (e - e0 + 1) * C].bitcast(FP8X4)
                 xgs[e] = scales[:, (e - e0) * C : (e - e0 + 1) * C]
 
-        def hidden(e):
-            pre = psum.tile([P, H], F32, name="pre")
+        def hidden(e, act_tag, pre_bank, turned_bank):
+            pre = psum.tile([P, H], F32, name="pre%d" % e, tag="bank%d" % pre_bank)
             nc.tensor.matmul_mx(
                 out=pre[:], lhsT=xg[e], lhsT_scale=xgs[e], rhs=wa_sb[e].bitcast(FP8X4),
                 rhs_scale=wa_plane[4 * e :, :], start=True, stop=True,
             )
-            act = ring.tile([P, H], BF16, name="act", align_bytes=64)
+            act[e] = keep.tile([P, H], BF16, name="act%d" % e, tag=act_tag, align_bytes=64)
             nc.scalar.activation(
-                act[:].rearrange("s (u p d) -> s u p d", u=2, d=2),
+                act[e][:].rearrange("s (u p d) -> s u p d", u=2, d=2),
                 pre[:].rearrange("s (p u d) -> s u p d", u=2, d=2),
                 GELU,
             )
-            turned = psum.tile([P, 2, C], F32, name="turned")
-            pairs = act[:].bitcast(F32)
+            turned[e] = psum.tile([P, 2, C], F32, name="turned%d" % e, tag="bank%d" % turned_bank)
+            pairs = act[e][:].bitcast(F32)
             for u in range(2):
-                nc.tensor.transpose(turned[:, u, :], pairs[:, u * P : (u + 1) * P], ident[:])
-            turned_ps[e] = turned
+                nc.tensor.transpose(turned[e][:, u, :], pairs[:, u * P : (u + 1) * P], ident[:])
 
-        def quantize_hidden(e, words):
-            nc.scalar.copy(words.rearrange("p (s u) -> p s u", u=2), turned_ps[e][:].rearrange("p u s -> p s u"))
-            codes = keep.tile([P, C], U32, name="hq%d" % e, align_bytes=64)
-            scales = keep.tile([P, C], U8, name="hqs%d" % e, align_bytes=64)
-            nc.vector.quantize_mx(out=codes[:].bitcast(FP8X4), scales=scales[:], in_=words.bitcast(BF16))
-            hq[e], hqs[e] = codes, scales
+        def hidden_in_halves(e, pre_banks, turned_bank):
+            act[e] = keep.tile([P, H], BF16, name="act%d" % e, align_bytes=64)
+            for a in range(2):
+                pre = psum.tile([P, HALF], F32, name="pre%d_%d" % (e, a), tag="bank%d" % pre_banks[a])
+                nc.tensor.matmul_mx(
+                    out=pre[:], lhsT=xg[e], lhsT_scale=xgs[e],
+                    rhs=wa_sb[e][:, a * HALF : (a + 1) * HALF].bitcast(FP8X4),
+                    rhs_scale=wa_plane[4 * e :, a * HALF : (a + 1) * HALF], start=True, stop=True,
+                )
+                nc.scalar.activation(
+                    act[e][:].rearrange("s (u p d) -> s u p d", u=2, d=2)[:, :, a * 64 : (a + 1) * 64, :],
+                    pre[:].rearrange("s (p u d) -> s u p d", u=2, d=2),
+                    GELU,
+                )
+            turned[e] = psum.tile([P, 2, C], F32, name="turned%d" % e, tag="bank%d" % turned_bank)
+            pairs = act[e][:].bitcast(F32)
+            for u in range(2):
+                nc.tensor.transpose(turned[e][:, u, :], pairs[:, u * P : (u + 1) * P], ident[:])
 
-        def quantize_wb(e, h, copy):
-            grouped = ring.tile([P, HALF * PACK], BF16, name="wb_grouped", align_bytes=64)
+        def quantize_hidden(e, copy, words, tag):
+            copy(words.rearrange("p (s u) -> p s u", u=2), turned[e][:].rearrange("p u s -> p s u"))
+            hq[e] = keep.tile([P, C], U32, name="hq%d" % e, tag=tag, align_bytes=64)
+            hqs[e] = keep.tile([P, C], U8, name="hqs%d" % e, align_bytes=64)
+            nc.vector.quantize_mx(out=hq[e][:].bitcast(FP8X4), scales=hqs[e][:], in_=words.bitcast(BF16))
+
+        def interleave(g, b, tag, copy, parts):
+            grouped[g, b] = keep.tile([P, 2 * P * PACK], BF16, name="grouped%d_%d" % (g, b), tag=tag, align_bytes=64)
+            dst = grouped[g, b][:].rearrange("p (e c i t) -> p e c t i", e=2, i=4, t=PACK)
+            cols = slice((b % 2) * P, (b % 2 + 1) * P)
+            src = wb_raw[g, b // 2][:, :, :, cols].rearrange("p e t (c i) -> p e c t i", i=4)
+            if parts == 1:
+                copy(dst, src)
+            else:
+                for m in range(2):
+                    copy(dst[:, m], src[:, m])
+
+        def quantize_wb(g, b):
+            codes = keep.tile([P, 2 * P], U32, name="wbq%d_%d" % (g, b), tag="codes%d_%d" % (g, b), align_bytes=64)
+            scales = keep.tile([P, 2 * P], U8, name="wbqs%d_%d" % (g, b), tag="scales%d_%d" % (g, b), align_bytes=64)
+            nc.vector.quantize_mx(out=codes[:].bitcast(FP8X4), scales=scales[:], in_=grouped[g, b][:])
+            for m in range(2):
+                wbq[2 * g + m, b] = codes[:, m * P : (m + 1) * P]
+                wbqs[2 * g + m, b] = scales[:, m * P : (m + 1) * P]
+
+        def interleave_half(e, h, copy, tag):
+            staged = keep.tile([P, HALF * PACK], BF16, name="staged%d_%d" % (e, h), tag=tag, align_bytes=64)
             copy(
-                grouped[:].rearrange("p (c i t) -> p c t i", i=4, t=PACK),
-                wb_raw[e, h].rearrange("p t (c i) -> p c t i", i=4),
+                staged[:].rearrange("p (c i t) -> p c t i", i=4, t=PACK),
+                raw_half(e, h).rearrange("p t (c i) -> p c t i", i=4),
             )
-            codes = keep.tile([P, HALF], U32, name="wbq%d_%d" % (e, h), align_bytes=64)
-            scales = keep.tile([P, HALF], U8, name="wbqs%d_%d" % (e, h), align_bytes=64)
-            nc.vector.quantize_mx(out=codes[:].bitcast(FP8X4), scales=scales[:], in_=grouped[:])
-            wbq[e, h], wbqs[e, h] = codes, scales
+            grouped[e, h, 0] = staged
 
-        def product(e, blocks, home):
-            acc = psum_y.tile([P, len(blocks), C], F32, name="acc")
-            for a, b in enumerate(blocks):
-                h, m0, n0 = b // 2, (b % 2) * P, b * P
+        def quantize_half(e, h, tag):
+            staged = grouped[e, h, 0]
+            codes = keep.tile([P, HALF], U32, name="hc%d_%d" % (e, h), tag=tag, align_bytes=64)
+            scales = keep.tile([P, HALF], U8, name="hs%d_%d" % (e, h), tag="hscales%d_%d" % (e, h), align_bytes=64)
+            nc.vector.quantize_mx(out=codes[:].bitcast(FP8X4), scales=scales[:], in_=staged[:])
+            for m in range(2):
+                wbq[e, 2 * h + m] = codes[:, m * P : (m + 1) * P]
+                wbqs[e, 2 * h + m] = scales[:, m * P : (m + 1) * P]
+
+        def unit(e0, e1, b, bank, home, store):
+            n0 = b * P
+            acc = psum.tile([P, e1 - e0, C], F32, name="acc%d_%d" % (e0, b), tag="bank%d" % bank)
+            for e in range(e0, e1):
+                nc.tensor.matmul_mx(
+                    out=acc[:, e - e0, :], lhsT=w_sb[e][:, 2 * n0 : 2 * (n0 + P)].bitcast(FP4X4),
+                    lhsT_scale=w_plane[:, e * N + n0 : e * N + n0 + P], rhs=xg[e], rhs_scale=xgs[e],
+                    start=True, stop=False,
+                )
+                nc.tensor.matmul_mx(
+                    out=acc[:, e - e0, :], lhsT=wbq[e, b].bitcast(FP8X4),
+                    lhsT_scale=wbqs[e, b], rhs=hq[e][:].bitcast(FP8X4),
+                    rhs_scale=hqs[e][:], start=False, stop=True,
+                )
+            nc.scalar.copy(home, acc[:].rearrange("p e s -> p (e s)"))
+            t, c0 = gate_sb[e0]
+            nc.vector.tensor_tensor(
+                windows[b][:].indirect(offsets[:, e0 * LIST_COLS : e1 * LIST_COLS]),
+                home,
+                t[:, c0 : c0 + (e1 - e0) * C],
+                MULT,
+            )
+            if store:
+                nc.sync.dma_start(out[b * P : (b + 1) * P, :], windows[b][:])
+
+        def unit_half(e, h, bank, home, store):
+            acc = psum.tile([P, 2, C], F32, name="acch%d_%d" % (e, h), tag="bank%d" % bank)
+            for a in range(2):
+                b = 2 * h + a
+                n0 = b * P
                 nc.tensor.matmul_mx(
                     out=acc[:, a, :], lhsT=w_sb[e][:, 2 * n0 : 2 * (n0 + P)].bitcast(FP4X4),
                     lhsT_scale=w_plane[:, e * N + n0 : e * N + n0 + P], rhs=xg[e], rhs_scale=xgs[e],
                     start=True, stop=False,
                 )
                 nc.tensor.matmul_mx(
-                    out=acc[:, a, :], lhsT=wbq[e, h][:, m0 : m0 + P].bitcast(FP8X4),
-                    lhsT_scale=wbqs[e, h][:, m0 : m0 + P], rhs=hq[e][:].bitcast(FP8X4),
+                    out=acc[:, a, :], lhsT=wbq[e, b].bitcast(FP8X4),
+                    lhsT_scale=wbqs[e, b], rhs=hq[e][:].bitcast(FP8X4),
                     rhs_scale=hqs[e][:], start=False, stop=True,
                 )
-            nc.scalar.copy(home, acc[:])
-
-        def scatter(e0, e1, b, values, store):
-            g0 = e0 - e0 % 2
-            nc.vector.tensor_tensor(
-                windows[b][:].indirect(offsets[:, e0 * LIST_COLS : e1 * LIST_COLS]),
-                values,
-                gate_sb[g0][:, (e0 - g0) * C : (e1 - g0) * C],
-                MULT,
-            )
-            if store:
-                nc.sync.dma_start(out[b * P : (b + 1) * P, :], windows[b][:])
-
-        def fresh(name, blocks):
-            return keep.tile([P, blocks, C], F32, name=name, align_bytes=64)[:]
-
-        def unit(e, h, home, store):
-            product(e, [2 * h, 2 * h + 1], home)
+            nc.scalar.copy(home, acc[:].rearrange("p e s -> p (e s)"))
+            t, c0 = gate_sb[e]
             for a in range(2):
-                scatter(e, e + 1, 2 * h + a, home[:, a, :], store)
+                b = 2 * h + a
+                nc.vector.tensor_tensor(
+                    windows[b][:].indirect(offsets[:, e * LIST_COLS : (e + 1) * LIST_COLS]),
+                    home[:, a * C : (a + 1) * C],
+                    t[:, c0 : c0 + C],
+                    MULT,
+                )
+                if store:
+                    nc.sync.dma_start(out[b * P : (b + 1) * P, :], windows[b][:])
 
-        def single(e, b, home):
-            product(e, [b], home)
-            scatter(e, e + 1, b, home[:, 0, :], False)
-
-        def spent(e, h, j):
-            return wb_raw[e, h][:, j, :].rearrange("p (a s) -> p a s", a=2)
+        def fresh(name, experts, tag=None):
+            return keep.tile([P, experts * C], F32, name=name, tag=tag or name, align_bytes=64)[:]
 
         gather(0, 1)
-        hidden(0)
+        hidden_in_halves(0, [0, 4], 1)
         gather(1, 2)
-        hidden(1)
+        hidden(1, "act1", 2, 7)
         gather(2, 4)
-        quantize_wb(0, 0, nc.vector.tensor_copy)
-        quantize_hidden(0, fresh("h0", 2).rearrange("p a s -> p (a s)"))
-        single(0, 0, fresh("y0", 1))
-        single(0, 1, fresh("y1", 1))
-        quantize_wb(0, 1, nc.vector.tensor_copy)
-        quantize_hidden(1, fresh("h1", 2).rearrange("p a s -> p (a s)"))
-        single(0, 2, fresh("y2", 1))
-        quantize_wb(1, 0, nc.scalar.copy)
-        single(0, 3, spent(1, 0, 0)[:, 0:1, :])
-        quantize_wb(1, 1, nc.scalar.copy)
-        unit(1, 0, spent(1, 1, 0), False)
-        hidden(2)
-        quantize_hidden(2, fresh("h2", 2).rearrange("p a s -> p (a s)"))
-        quantize_wb(2, 0, nc.scalar.copy)
-        unit(1, 1, spent(2, 0, 0), False)
-        hidden(3)
-        quantize_wb(3, 0, nc.scalar.copy)
-        quantize_hidden(3, wb_raw[3, 0][:, 1, :])
-        unit(2, 0, spent(3, 0, 0), False)
-        quantize_wb(2, 1, nc.scalar.copy)
-        quantize_wb(3, 1, nc.scalar.copy)
-        unit(3, 0, spent(3, 1, 0), True)
-        last = wb_raw[3, 1][:, 1:3, :]
-        product(2, [2, 3], last[:, :, :C])
-        product(3, [2, 3], last[:, :, C:])
-        for a in range(2):
-            scatter(2, 4, 2 + a, last[:, a, :], True)
+        interleave_half(0, 0, nc.vector.tensor_copy, "s00")
+        quantize_half(0, 0, "hcodes0_0")
+        quantize_hidden(0, nc.scalar.copy, fresh("h0", 2), "hq0")
+        interleave_half(0, 1, nc.vector.tensor_copy, "s01")
+        quantize_half(0, 1, "hcodes0_1")
+        quantize_hidden(1, nc.scalar.copy, fresh("h1", 2), "hq1")
+        y0 = fresh("y0", 1)
+        unit(0, 1, 0, 5, y0, False)
+        unit(0, 1, 1, 6, fresh("y0b", 1), False)
+        interleave_half(1, 0, nc.scalar.copy, "hcodes0_0")
+        quantize_half(1, 0, "hcodes1_0")
+        unit_half(0, 1, 3, wb_own[1, 0][:, 0, :], False)
+        interleave_half(1, 1, nc.scalar.copy, "hcodes0_0")
+        quantize_half(1, 1, "hcodes1_1")
+        y10 = fresh("y10", 2)
+        unit_half(1, 0, 4, y10, False)
+        hidden(2, "hscales1_0", 3, 1)
+        interleave_half(2, 0, nc.scalar.copy, "hcodes1_0")
+        quantize_half(2, 0, "hcodes2_0")
+        quantize_hidden(2, nc.scalar.copy, fresh("h2", 2), "hq2")
+        y11 = fresh("y11", 2)
+        unit_half(1, 1, 5, y11, False)
+        hidden(3, "hscales1_1", 4, 2)
+        interleave_half(3, 0, nc.scalar.copy, "hcodes1_1")
+        quantize_half(3, 0, "hcodes3_0")
+        quantize_hidden(3, nc.scalar.copy, fresh("h3", 2), "hq3")
+        y20 = fresh("y20", 2)
+        unit_half(2, 0, 6, y20, False)
+        interleave(1, 2, "hcodes2_0", nc.scalar.copy, 1)
+        quantize_wb(1, 2)
+        unit_half(3, 0, 7, wb_flat[1, 1][:, : 2 * C], True)
+        interleave(1, 3, "hcodes3_0", nc.scalar.copy, 1)
+        quantize_wb(1, 3)
+        unit(2, 4, 2, 0, fresh("y2", 2), True)
+        unit(2, 4, 3, 1, fresh("y3", 2), True)

@@ -126,12 +126,14 @@ def tile_moe_elr_gelu_kernel(
         load_wa(1, 2)
         load_wb(0, 0)
         load_wb(0, 1)
-        load_w(0, 2)
+        load_w(0, 1)
         for r in range(4):
             load_w_scales(r, nc.sync)
+        load_gate(0, 1)
         load_wb(1, 0)
-        load_gate(0, 2)
+        load_gate(1, 2)
         load_wb(1, 1)
+        load_w(1, 2)
         load_wa(2, 3)
         load_wb(2, 0)
         load_wa(3, 4)
@@ -312,7 +314,7 @@ def tile_moe_elr_gelu_kernel(
         interleave_half(2, 0, nc.scalar.copy, "hcodes1_0")
         quantize_half(2, 0, "hcodes2_0")
         quantize_hidden(2, nc.scalar.copy, fresh("h2", 2), "hq2")
-        y11 = fresh("y11", 2)
+        y11 = wb_own[2, 0][:, 0, :]
         unit_half(1, 1, 5, y11, False)
         hidden(3, "hscales1_1", 4, 2)
         interleave_half(3, 0, nc.scalar.copy, "hcodes1_1")

@@ -35,37 +35,24 @@ def tile_moe_elr_gelu_kernel(
         x_tab = keep.tile([P, T], U32, name="x_tab", align_bytes=64)
         xs_tab = keep.tile([P, T], U8, name="xs_tab", align_bytes=64)
         wa_plane = keep.tile([P, H], U8, name="wa_plane", align_bytes=64)
-        w_plane = keep.tile([P, E * N], U8, name="w_plane", align_bytes=64)
         windows = [keep.tile([P, T], F32, name="window%d" % b) for b in range(N // P)]
         ident = keep.tile([P, P], F32, name="ident")
-        wb_flat = {
-            (g, h): keep.tile([P, P + 2 * PACK * HALF], F32, name="wb%d_%d" % (g, h), align_bytes=64)
-            for g in range(2)
-            for h in range(2)
-            if (g, h) == (1, 1)
-        }
-        wb_raw = {key: t[:, P:].rearrange("p (e j n) -> p e j n", e=2, j=PACK) for key, t in wb_flat.items()}
-        wb_own = {
-            (e, h): keep.tile([P, PACK, HALF], F32, name="own%d_%d" % (e, h), tag="own%d_%d" % (e, h), align_bytes=64)
-            for e in range(E)
-            for h in range(2)
-            if e < 2 or h == 0
-        }
-
-        def raw_half(e, h):
-            return wb_own[e, h][:] if (e, h) in wb_own else wb_raw[e // 2, h][:, e % 2]
-
         zero = keep.tile([P, 8], F32, name="zero")
+        w_planes = {
+            e0: keep.tile([P, (e1 - e0) * N], U8, name="w_plane%d" % e0, align_bytes=64) for e0, e1 in ((0, 2), (2, 4))
+        }
+
         nc.vector.memset(wa_plane[:].bitcast(I32), 0)
         nc.vector.memset(zero[:], 0.0)
-        nc.vector.memset(w_plane[:].bitcast(I32), 0)
+        for plane in w_planes.values():
+            nc.vector.memset(plane[:].bitcast(I32), 0)
         for b in range(2):
             nc.vector.memset(windows[b][:], 0.0)
         for b in range(2, 4):
             nc.scalar.activation(windows[b][:], zero[:, 0:1].to_broadcast([P, T]), GELU)
         make_identity(nc, ident[:])
 
-        wa_sb, w_sb, gate_sb = {}, {}, {}
+        wa_sb, w_sb, ws_sb, gate_sb, raw, flat = {}, {}, {}, {}, {}, {}
 
         def load_x():
             nc.sync.dma_start(x_tab[:].bitcast(I32), x_words[0].rearrange("p t d -> p (t d)").bitcast(I32))
@@ -76,25 +63,24 @@ def tile_moe_elr_gelu_kernel(
                 xs_tab[32 * q : 32 * q + 32, :].bitcast(I32), rows.unsqueeze(0).to_broadcast([8, 4, T // 4])
             )
 
-        def load_wa_scales(q, queue):
-            queue.dma_start(
+        def load_wa_scales(q):
+            nc.sync.dma_start(
                 wa_plane[32 * q : 32 * q + 16, :].bitcast(I32), wa_scales[:, 0, 4 * q : 4 * q + 4, :].bitcast(I32)
             )
 
-        def load_w_scales(r, queue):
-            queue.dma_start(
-                w_plane[r:P:32, :].bitcast(I32).rearrange("q (e n) -> q e n", e=E),
-                w_scales[:, 0, r:16:4, :].rearrange("e q n -> q e n").bitcast(I32),
-            )
-
-        def load_wa(e0, e1):
-            t = keep.tile([P, (e1 - e0) * H], U32, name="wa%d" % e0, align_bytes=64)
-            nc.sync.dma_start(
-                t[:].bitcast(I32).rearrange("p (e i) -> p e i", i=H),
-                wa_words[e0:e1, 0].rearrange("e p i d -> p e (i d)").bitcast(I32),
-            )
+        def load_w_scales(e0, e1):
+            for r in range(4):
+                nc.sync.dma_start(
+                    w_planes[e0][r:P:32, :].bitcast(I32).rearrange("q (e n) -> q e n", e=e1 - e0),
+                    w_scales[e0:e1, 0, r:16:4, :].rearrange("e q n -> q e n").bitcast(I32),
+                )
             for e in range(e0, e1):
-                wa_sb[e] = t[:, (e - e0) * H : (e - e0 + 1) * H]
+                ws_sb[e] = w_planes[e0][:, (e - e0) * N : (e - e0 + 1) * N]
+
+        def load_wa(e):
+            t = keep.tile([P, H], U32, name="wa%d" % e, align_bytes=64)
+            nc.sync.dma_start(t[:].bitcast(I32), wa_words[e, 0].rearrange("p i d -> p (i d)").bitcast(I32))
+            wa_sb[e] = t[:]
 
         def load_w(e0, e1):
             t = keep.tile([P, (e1 - e0) * 2 * N], U8, name="w%d" % e0, align_bytes=64)
@@ -105,45 +91,42 @@ def tile_moe_elr_gelu_kernel(
             for e in range(e0, e1):
                 w_sb[e] = t[:, (e - e0) * 2 * N : (e - e0 + 1) * 2 * N]
 
-        def load_gate(e0, e1):
-            t = keep.tile([P, (e1 - e0) * C], F32, name="gate%d" % e0)
-            nc.sync.dma_start(t[:], gate[:, e0 * C : e1 * C])
-            for e in range(e0, e1):
-                gate_sb[e] = (t, (e - e0) * C)
-
-        def load_wb(e, h):
-            nc.sync.dma_start(
-                raw_half(e, h), wb[e, :, h * HALF : (h + 1) * HALF].rearrange("(p j) n -> p j n", j=PACK)
-            )
+        def load_wb_half(e, h):
+            t = keep.tile([P, PACK * HALF], F32, name="wb%d_%d" % (e, h), align_bytes=64)
+            raw[e, h] = t[:].rearrange("p (j n) -> p j n", j=PACK)
+            nc.sync.dma_start(raw[e, h], wb[e, :, h * HALF : (h + 1) * HALF].rearrange("(p j) n -> p j n", j=PACK))
+            flat[e, h] = t
 
         nc.sync.dma_start(offsets[:], offs)
+        gate_col = keep.tile([P, PACK], F32, name="gate_col")
+        nc.sync.dma_start(gate_col[:], gate[0].rearrange("(p j) -> p j", j=PACK))
         for q in range(4):
             load_x_scales(q)
         load_x()
-        load_wa(0, 1)
+        load_wa(0)
         for q in range(4):
-            load_wa_scales(q, nc.sync)
-        load_wa(1, 2)
-        load_wb(0, 0)
-        load_wb(0, 1)
+            load_wa_scales(q)
+        load_wa(1)
+        load_wb_half(0, 0)
+        load_w_scales(0, 2)
+        load_wb_half(0, 1)
         load_w(0, 1)
-        for r in range(4):
-            load_w_scales(r, nc.sync)
-        load_gate(0, 1)
-        load_wb(1, 0)
-        load_gate(1, 2)
-        load_wb(1, 1)
+        load_wb_half(1, 0)
+        load_wb_half(1, 1)
         load_w(1, 2)
-        load_wa(2, 3)
-        load_wb(2, 0)
-        load_wa(3, 4)
-        load_wb(3, 0)
-        load_w(2, 4)
-        load_wb(2, 1)
-        load_wb(3, 1)
-        load_gate(2, 4)
+        load_wa(2)
+        load_wb_half(2, 0)
+        load_wa(3)
+        load_wb_half(3, 0)
+        load_w_scales(2, 4)
+        load_w(2, 3)
+        last = keep.tile([P, P + 2 * PACK * HALF], F32, name="wb_last", align_bytes=64)
+        last_raw = last[:, P:].rearrange("p (e j n) -> p e j n", e=2, j=PACK)
+        for e in (2, 3):
+            nc.sync.dma_start(last_raw[:, e - 2], wb[e, :, HALF:].rearrange("(p j) n -> p j n", j=PACK))
+        load_w(3, 4)
 
-        xg, xgs, act, turned, hq, hqs, grouped, wbq, wbqs = {}, {}, {}, {}, {}, {}, {}, {}, {}
+        xg, xgs, act, turned, hq, hqs, staged, wbq, wbqs = {}, {}, {}, {}, {}, {}, {}, {}, {}
 
         def gather(e0, e1):
             lst = offsets[:, e0 * LIST_COLS : e1 * LIST_COLS]
@@ -155,177 +138,160 @@ def tile_moe_elr_gelu_kernel(
                 xg[e] = words[:, (e - e0) * C : (e - e0 + 1) * C].bitcast(FP8X4)
                 xgs[e] = scales[:, (e - e0) * C : (e - e0 + 1) * C]
 
-        def hidden(e, act_tag, pre_bank, turned_bank):
-            pre = psum.tile([P, H], F32, name="pre%d" % e, tag="bank%d" % pre_bank)
-            nc.tensor.matmul_mx(
-                out=pre[:], lhsT=xg[e], lhsT_scale=xgs[e], rhs=wa_sb[e].bitcast(FP8X4),
-                rhs_scale=wa_plane[4 * e :, :], start=True, stop=True,
-            )
+        def hidden(e, act_tag, pre_banks):
             act[e] = keep.tile([P, H], BF16, name="act%d" % e, tag=act_tag, align_bytes=64)
-            nc.scalar.activation(
-                act[e][:].rearrange("s (u p d) -> s u p d", u=2, d=2),
-                pre[:].rearrange("s (p u d) -> s u p d", u=2, d=2),
-                GELU,
-            )
-            turned[e] = psum.tile([P, 2, C], F32, name="turned%d" % e, tag="bank%d" % turned_bank)
-            pairs = act[e][:].bitcast(F32)
-            for u in range(2):
-                nc.tensor.transpose(turned[e][:, u, :], pairs[:, u * P : (u + 1) * P], ident[:])
-
-        def hidden_in_halves(e, pre_banks, turned_bank):
-            act[e] = keep.tile([P, H], BF16, name="act%d" % e, align_bytes=64)
-            for a in range(2):
-                pre = psum.tile([P, HALF], F32, name="pre%d_%d" % (e, a), tag="bank%d" % pre_banks[a])
+            width = H // len(pre_banks)
+            for a, bank in enumerate(pre_banks):
+                cols = slice(a * width, (a + 1) * width)
+                pre = psum.tile([P, width], F32, name="pre%d_%d" % (e, a), tag="bank%d" % bank)
                 nc.tensor.matmul_mx(
-                    out=pre[:], lhsT=xg[e], lhsT_scale=xgs[e],
-                    rhs=wa_sb[e][:, a * HALF : (a + 1) * HALF].bitcast(FP8X4),
-                    rhs_scale=wa_plane[4 * e :, a * HALF : (a + 1) * HALF], start=True, stop=True,
+                    out=pre[:], lhsT=xg[e], lhsT_scale=xgs[e], rhs=wa_sb[e][:, cols].bitcast(FP8X4),
+                    rhs_scale=wa_plane[4 * e :, cols], start=True, stop=True,
                 )
                 nc.scalar.activation(
-                    act[e][:].rearrange("s (u p d) -> s u p d", u=2, d=2)[:, :, a * 64 : (a + 1) * 64, :],
+                    act[e][:].rearrange("s (u p d) -> s u p d", u=2, d=2)[:, :, a * width // 4 : (a + 1) * width // 4, :],
                     pre[:].rearrange("s (p u d) -> s u p d", u=2, d=2),
                     GELU,
                 )
+
+        def turn(e, turned_bank):
             turned[e] = psum.tile([P, 2, C], F32, name="turned%d" % e, tag="bank%d" % turned_bank)
             pairs = act[e][:].bitcast(F32)
             for u in range(2):
                 nc.tensor.transpose(turned[e][:, u, :], pairs[:, u * P : (u + 1) * P], ident[:])
 
-        def quantize_hidden(e, copy, words, tag):
-            copy(words.rearrange("p (s u) -> p s u", u=2), turned[e][:].rearrange("p u s -> p s u"))
-            hq[e] = keep.tile([P, C], U32, name="hq%d" % e, tag=tag, align_bytes=64)
+        def quantize_hidden(e, words):
+            nc.scalar.copy(words.rearrange("p (s u) -> p s u", u=2), turned[e][:].rearrange("p u s -> p s u"))
+            hq[e] = keep.tile([P, C], U32, name="hq%d" % e, align_bytes=64)
             hqs[e] = keep.tile([P, C], U8, name="hqs%d" % e, align_bytes=64)
             nc.vector.quantize_mx(out=hq[e][:].bitcast(FP8X4), scales=hqs[e][:], in_=words.bitcast(BF16))
 
-        def interleave(g, b, tag, copy, parts):
-            grouped[g, b] = keep.tile([P, 2 * P * PACK], BF16, name="grouped%d_%d" % (g, b), tag=tag, align_bytes=64)
-            dst = grouped[g, b][:].rearrange("p (e c i t) -> p e c t i", e=2, i=4, t=PACK)
-            cols = slice((b % 2) * P, (b % 2 + 1) * P)
-            src = wb_raw[g, b // 2][:, :, :, cols].rearrange("p e t (c i) -> p e c t i", i=4)
-            if parts == 1:
-                copy(dst, src)
-            else:
-                for m in range(2):
-                    copy(dst[:, m], src[:, m])
+        def interleave(key, parts, copy, tag):
+            staged[key] = keep.tile([P, HALF * PACK], BF16, name="staged%s" % key, tag=tag, align_bytes=64)
+            at = 0
+            for part in parts:
+                width = part.shape[2]
+                copy(
+                    staged[key][:, at * PACK : (at + width) * PACK].rearrange("p (c i t) -> p c t i", i=4, t=PACK),
+                    part.rearrange("p t (c i) -> p c t i", i=4),
+                )
+                at = at + width
 
-        def quantize_wb(g, b):
-            codes = keep.tile([P, 2 * P], U32, name="wbq%d_%d" % (g, b), tag="codes%d_%d" % (g, b), align_bytes=64)
-            scales = keep.tile([P, 2 * P], U8, name="wbqs%d_%d" % (g, b), tag="scales%d_%d" % (g, b), align_bytes=64)
-            nc.vector.quantize_mx(out=codes[:].bitcast(FP8X4), scales=scales[:], in_=grouped[g, b][:])
-            for m in range(2):
-                wbq[2 * g + m, b] = codes[:, m * P : (m + 1) * P]
-                wbqs[2 * g + m, b] = scales[:, m * P : (m + 1) * P]
-
-        def interleave_half(e, h, copy, tag):
-            staged = keep.tile([P, HALF * PACK], BF16, name="staged%d_%d" % (e, h), tag=tag, align_bytes=64)
-            copy(
-                staged[:].rearrange("p (c i t) -> p c t i", i=4, t=PACK),
-                raw_half(e, h).rearrange("p t (c i) -> p c t i", i=4),
+        def interleave_pair(key, part, tag):
+            staged[key] = keep.tile([P, HALF * PACK], BF16, name="staged%s" % key, tag=tag, align_bytes=64)
+            nc.scalar.copy(
+                staged[key][:].rearrange("p (e c i t) -> p e c t i", e=2, i=4, t=PACK),
+                part.rearrange("p e t (c i) -> p e c t i", i=4),
             )
-            grouped[e, h, 0] = staged
 
-        def quantize_half(e, h, tag):
-            staged = grouped[e, h, 0]
-            codes = keep.tile([P, HALF], U32, name="hc%d_%d" % (e, h), tag=tag, align_bytes=64)
-            scales = keep.tile([P, HALF], U8, name="hs%d_%d" % (e, h), tag="hscales%d_%d" % (e, h), align_bytes=64)
-            nc.vector.quantize_mx(out=codes[:].bitcast(FP8X4), scales=scales[:], in_=staged[:])
-            for m in range(2):
-                wbq[e, 2 * h + m] = codes[:, m * P : (m + 1) * P]
-                wbqs[e, 2 * h + m] = scales[:, m * P : (m + 1) * P]
+        def quantize_wb(key, blocks):
+            codes = keep.tile([P, HALF], U32, name="codes%s" % key, tag="codes%s" % key, align_bytes=64)
+            scales = keep.tile([P, HALF], U8, name="scales%s" % key, tag="scales%s" % key, align_bytes=64)
+            nc.vector.quantize_mx(out=codes[:].bitcast(FP8X4), scales=scales[:], in_=staged[key][:])
+            for m, eb in enumerate(blocks):
+                wbq[eb] = codes[:, m * P : (m + 1) * P]
+                wbqs[eb] = scales[:, m * P : (m + 1) * P]
 
-        def unit(e0, e1, b, bank, home, store):
-            n0 = b * P
-            acc = psum.tile([P, e1 - e0, C], F32, name="acc%d_%d" % (e0, b), tag="bank%d" % bank)
-            for e in range(e0, e1):
+        def products(blocks, bank):
+            acc = psum.tile([P, len(blocks), C], F32, name="acc%d_%d" % blocks[0], tag="bank%d" % bank)
+            for m, (e, b) in enumerate(blocks):
+                n0 = b * P
                 nc.tensor.matmul_mx(
-                    out=acc[:, e - e0, :], lhsT=w_sb[e][:, 2 * n0 : 2 * (n0 + P)].bitcast(FP4X4),
-                    lhsT_scale=w_plane[:, e * N + n0 : e * N + n0 + P], rhs=xg[e], rhs_scale=xgs[e],
-                    start=True, stop=False,
+                    out=acc[:, m, :], lhsT=w_sb[e][:, 2 * n0 : 2 * (n0 + P)].bitcast(FP4X4),
+                    lhsT_scale=ws_sb[e][:, n0 : n0 + P], rhs=xg[e], rhs_scale=xgs[e], start=True, stop=False,
                 )
                 nc.tensor.matmul_mx(
-                    out=acc[:, e - e0, :], lhsT=wbq[e, b].bitcast(FP8X4),
-                    lhsT_scale=wbqs[e, b], rhs=hq[e][:].bitcast(FP8X4),
-                    rhs_scale=hqs[e][:], start=False, stop=True,
+                    out=acc[:, m, :], lhsT=wbq[e, b].bitcast(FP8X4), lhsT_scale=wbqs[e, b],
+                    rhs=hq[e][:].bitcast(FP8X4), rhs_scale=hqs[e][:], start=False, stop=True,
                 )
-            nc.scalar.copy(home, acc[:].rearrange("p e s -> p (e s)"))
+            return acc
+
+        def leave(acc, home):
+            nc.scalar.copy(home, acc[:].rearrange("p m s -> p (m s)"))
+
+        def scatter(e0, e1, b, values, store):
             t, c0 = gate_sb[e0]
             nc.vector.tensor_tensor(
                 windows[b][:].indirect(offsets[:, e0 * LIST_COLS : e1 * LIST_COLS]),
-                home,
-                t[:, c0 : c0 + (e1 - e0) * C],
-                MULT,
+                values, t[:, c0 : c0 + (e1 - e0) * C], MULT,
             )
             if store:
                 nc.sync.dma_start(out[b * P : (b + 1) * P, :], windows[b][:])
 
-        def unit_half(e, h, bank, home, store):
-            acc = psum.tile([P, 2, C], F32, name="acch%d_%d" % (e, h), tag="bank%d" % bank)
-            for a in range(2):
-                b = 2 * h + a
-                n0 = b * P
-                nc.tensor.matmul_mx(
-                    out=acc[:, a, :], lhsT=w_sb[e][:, 2 * n0 : 2 * (n0 + P)].bitcast(FP4X4),
-                    lhsT_scale=w_plane[:, e * N + n0 : e * N + n0 + P], rhs=xg[e], rhs_scale=xgs[e],
-                    start=True, stop=False,
-                )
-                nc.tensor.matmul_mx(
-                    out=acc[:, a, :], lhsT=wbq[e, b].bitcast(FP8X4),
-                    lhsT_scale=wbqs[e, b], rhs=hq[e][:].bitcast(FP8X4),
-                    rhs_scale=hqs[e][:], start=False, stop=True,
-                )
-            nc.scalar.copy(home, acc[:].rearrange("p e s -> p (e s)"))
-            t, c0 = gate_sb[e]
-            for a in range(2):
-                b = 2 * h + a
-                nc.vector.tensor_tensor(
-                    windows[b][:].indirect(offsets[:, e * LIST_COLS : (e + 1) * LIST_COLS]),
-                    home[:, a * C : (a + 1) * C],
-                    t[:, c0 : c0 + C],
-                    MULT,
-                )
-                if store:
-                    nc.sync.dma_start(out[b * P : (b + 1) * P, :], windows[b][:])
+        def half_products(e, h, bank):
+            return products([(e, 2 * h), (e, 2 * h + 1)], bank)
 
-        def fresh(name, experts, tag=None):
-            return keep.tile([P, experts * C], F32, name=name, tag=tag or name, align_bytes=64)[:]
+        def half_scatter(e, h, home, store):
+            for a in range(2):
+                scatter(e, e + 1, 2 * h + a, home[:, a * C : (a + 1) * C], store)
 
+        def fresh(name, width):
+            return keep.tile([P, width], F32, name=name, align_bytes=64)[:]
+
+        spread = psum.tile([P, PACK, P], F32, name="spread", tag="bank5")
+        for j in range(PACK):
+            nc.tensor.transpose(spread[:, j, :], gate_col[:, j : j + 1].to_broadcast([P, P]), ident[:])
+        gates = keep.tile([P, E * C], F32, name="gates")
+        nc.scalar.copy(gates[:].rearrange("p (n j) -> p n j", j=PACK), spread[:].rearrange("p j n -> p n j"))
+        for e in range(E):
+            gate_sb[e] = (gates, e * C)
         gather(0, 1)
-        hidden_in_halves(0, [0, 4], 1)
+        hidden(0, "act0", [0, 4])
+        turn(0, 1)
         gather(1, 2)
-        hidden(1, "act1", 2, 7)
+        hidden(1, "act1", [2])
+        turn(1, 7)
         gather(2, 4)
-        interleave_half(0, 0, nc.vector.tensor_copy, "s00")
-        quantize_half(0, 0, "hcodes0_0")
-        quantize_hidden(0, nc.scalar.copy, fresh("h0", 2), "hq0")
-        interleave_half(0, 1, nc.vector.tensor_copy, "s01")
-        quantize_half(0, 1, "hcodes0_1")
-        quantize_hidden(1, nc.scalar.copy, fresh("h1", 2), "hq1")
-        y0 = fresh("y0", 1)
-        unit(0, 1, 0, 5, y0, False)
-        unit(0, 1, 1, 6, fresh("y0b", 1), False)
-        interleave_half(1, 0, nc.scalar.copy, "hcodes0_0")
-        quantize_half(1, 0, "hcodes1_0")
-        unit_half(0, 1, 3, wb_own[1, 0][:, 0, :], False)
-        interleave_half(1, 1, nc.scalar.copy, "hcodes0_0")
-        quantize_half(1, 1, "hcodes1_1")
-        y10 = fresh("y10", 2)
-        unit_half(1, 0, 4, y10, False)
-        hidden(2, "hscales1_0", 3, 1)
-        interleave_half(2, 0, nc.scalar.copy, "hcodes1_0")
-        quantize_half(2, 0, "hcodes2_0")
-        quantize_hidden(2, nc.scalar.copy, fresh("h2", 2), "hq2")
-        y11 = wb_own[2, 0][:, 0, :]
-        unit_half(1, 1, 5, y11, False)
-        hidden(3, "hscales1_1", 4, 2)
-        interleave_half(3, 0, nc.scalar.copy, "hcodes1_1")
-        quantize_half(3, 0, "hcodes3_0")
-        quantize_hidden(3, nc.scalar.copy, fresh("h3", 2), "hq3")
-        y20 = fresh("y20", 2)
-        unit_half(2, 0, 6, y20, False)
-        interleave(1, 2, "hcodes2_0", nc.scalar.copy, 1)
-        quantize_wb(1, 2)
-        unit_half(3, 0, 7, wb_flat[1, 1][:, : 2 * C], True)
-        interleave(1, 3, "hcodes3_0", nc.scalar.copy, 1)
-        quantize_wb(1, 3)
-        unit(2, 4, 2, 0, fresh("y2", 2), True)
-        unit(2, 4, 3, 1, fresh("y3", 2), True)
+        interleave("00", [raw[0, 0]], nc.vector.tensor_copy, "s00")
+        quantize_wb("00", [(0, 0), (0, 1)])
+        quantize_hidden(0, fresh("h0", 2 * C))
+        interleave("01", [raw[0, 1]], nc.vector.tensor_copy, "h0")
+        quantize_wb("01", [(0, 2), (0, 3)])
+        quantize_hidden(1, fresh("h1", 2 * C))
+        y0 = fresh("y0", C)
+        leave(products([(0, 0)], 5), y0)
+        scatter(0, 1, 0, y0, False)
+        y0b = fresh("y0b", C)
+        leave(products([(0, 1)], 6), y0b)
+        scatter(0, 1, 1, y0b, False)
+        interleave("10", [raw[1, 0]], nc.scalar.copy, "codes00")
+        quantize_wb("10", [(1, 0), (1, 1)])
+        y01 = flat[1, 0][:, :HALF]
+        leave(half_products(0, 1, 3), y01)
+        half_scatter(0, 1, y01, False)
+        interleave("11", [raw[1, 1][:, :, :64], raw[1, 1][:, :, 64:]], nc.scalar.copy, "s00")
+        quantize_wb("11", [(1, 2), (1, 3)])
+        y10 = fresh("y10", 2 * C)
+        leave(half_products(1, 0, 4), y10)
+        half_scatter(1, 0, y10, False)
+        hidden(2, "scales10", [0, 3])
+        interleave("20", [raw[2, 0]], nc.scalar.copy, "codes10")
+        quantize_wb("20", [(2, 0), (2, 1)])
+        acc11 = half_products(1, 1, 5)
+        turn(2, 1)
+        quantize_hidden(2, fresh("h2", 2 * C))
+        y11 = flat[2, 0][:, :HALF]
+        leave(acc11, y11)
+        half_scatter(1, 1, y11, False)
+        hidden(3, "scales11", [4])
+        interleave("30", [raw[3, 0]], nc.scalar.copy, "codes11")
+        quantize_wb("30", [(3, 0), (3, 1)])
+        acc20 = half_products(2, 0, 6)
+        turn(3, 2)
+        quantize_hidden(3, fresh("h3", 2 * C))
+        y20 = flat[3, 0][:, :HALF]
+        leave(acc20, y20)
+        half_scatter(2, 0, y20, False)
+        interleave_pair("b2", last_raw[:, :, :, :P], "codes20")
+        quantize_wb("b2", [(2, 2), (3, 2)])
+        y30 = last[:, : 2 * C]
+        leave(half_products(3, 0, 7), y30)
+        half_scatter(3, 0, y30, True)
+        interleave_pair("b3", last_raw[:, :, :, P:], "codes20")
+        quantize_wb("b3", [(2, 3), (3, 3)])
+        y2 = fresh("y2", 2 * C)
+        leave(products([(2, 2), (3, 2)], 0), y2)
+        scatter(2, 4, 2, y2, True)
+        y3 = fresh("y3", 2 * C)
+        leave(products([(2, 3), (3, 3)], 1), y3)
+        scatter(2, 4, 3, y3, True)

@@ -15,6 +15,7 @@ U8 = mybir.dt.uint8
 FP8X4 = mybir.dt.float8_e4m3fn_x4
 FP4X4 = mybir.dt.float4_e2m1fn_x4
 GELU = mybir.ActivationFunctionType.Gelu_apprx_tanh
+COPY = mybir.ActivationFunctionType.Copy
 MULT = mybir.AluOpType.mult
 
 P = 128
@@ -39,7 +40,7 @@ def tile_moe_elr_gelu_kernel(
         ident = keep.tile([P, P], F32, name="ident")
         zero = keep.tile([P, 8], F32, name="zero")
         w_planes = {
-            e0: keep.tile([P, (e1 - e0) * N], U8, name="w_plane%d" % e0, align_bytes=64) for e0, e1 in ((0, 2), (2, 4))
+            e0: keep.tile([P, 2 * N], U8, name="w_plane%d" % e0, align_bytes=64) for e0 in (0, 2)
         }
 
         nc.vector.memset(wa_plane[:].bitcast(I32), 0)
@@ -50,83 +51,69 @@ def tile_moe_elr_gelu_kernel(
             nc.vector.memset(windows[b][:], 0.0)
         for b in range(2, 4):
             nc.scalar.activation(windows[b][:], zero[:, 0:1].to_broadcast([P, T]), GELU)
-        make_identity(nc, ident[:])
 
-        wa_sb, w_sb, ws_sb, gate_sb, raw, flat = {}, {}, {}, {}, {}, {}
+        wa_sb, w_sb, ws_sb, raw = {}, {}, {}, {}
 
-        def load_x():
-            nc.sync.dma_start(x_tab[:].bitcast(I32), x_words[0].rearrange("p t d -> p (t d)").bitcast(I32))
-
-        def load_x_scales(q):
-            rows = x_scales[0, 4 * q : 4 * q + 4, :].bitcast(I32)
-            nc.sync.dma_start(
-                xs_tab[32 * q : 32 * q + 32, :].bitcast(I32), rows.unsqueeze(0).to_broadcast([8, 4, T // 4])
-            )
-
-        def load_wa_scales(q):
-            nc.sync.dma_start(
-                wa_plane[32 * q : 32 * q + 16, :].bitcast(I32), wa_scales[:, 0, 4 * q : 4 * q + 4, :].bitcast(I32)
-            )
-
-        def load_w_scales(e0, e1):
+        def load_w_scales(e0):
             for r in range(4):
                 nc.sync.dma_start(
-                    w_planes[e0][r:P:32, :].bitcast(I32).rearrange("q (e n) -> q e n", e=e1 - e0),
-                    w_scales[e0:e1, 0, r:16:4, :].rearrange("e q n -> q e n").bitcast(I32),
+                    w_planes[e0][r:P:32, :].bitcast(I32).rearrange("q (e n) -> q e n", e=2),
+                    w_scales[e0 : e0 + 2, 0, r:16:4, :].rearrange("e q n -> q e n").bitcast(I32),
                 )
-            for e in range(e0, e1):
+            for e in range(e0, e0 + 2):
                 ws_sb[e] = w_planes[e0][:, (e - e0) * N : (e - e0 + 1) * N]
 
-        def load_wa(e):
-            t = keep.tile([P, H], U32, name="wa%d" % e, align_bytes=64)
-            nc.sync.dma_start(t[:].bitcast(I32), wa_words[e, 0].rearrange("p i d -> p (i d)").bitcast(I32))
-            wa_sb[e] = t[:]
-
-        def load_w(e0, e1):
-            t = keep.tile([P, (e1 - e0) * 2 * N], U8, name="w%d" % e0, align_bytes=64)
+        def load_wa(e0, e1):
+            t = keep.tile([P, (e1 - e0) * H], U32, name="wa%d" % e0, align_bytes=64)
             nc.sync.dma_start(
-                t[:].bitcast(I32).rearrange("p (e n) -> p e n", e=e1 - e0),
-                w_words[e0:e1, 0].rearrange("e p n -> p e n").bitcast(I32),
+                t[:].bitcast(I32).rearrange("p (e i) -> p e i", e=e1 - e0),
+                wa_words[e0:e1, 0].rearrange("e p i d -> p e (i d)").bitcast(I32),
             )
             for e in range(e0, e1):
-                w_sb[e] = t[:, (e - e0) * 2 * N : (e - e0 + 1) * 2 * N]
+                wa_sb[e] = t[:, (e - e0) * H : (e - e0 + 1) * H]
 
-        def load_wb_half(e, h):
+        def load_w(e):
+            t = keep.tile([P, 2 * N], U8, name="w%d" % e, align_bytes=64)
+            nc.sync.dma_start(t[:].bitcast(I32), w_words[e, 0].bitcast(I32))
+            w_sb[e] = t[:]
+
+        def load_wb(e, h):
             t = keep.tile([P, PACK * HALF], F32, name="wb%d_%d" % (e, h), align_bytes=64)
             raw[e, h] = t[:].rearrange("p (j n) -> p j n", j=PACK)
             nc.sync.dma_start(raw[e, h], wb[e, :, h * HALF : (h + 1) * HALF].rearrange("(p j) n -> p j n", j=PACK))
-            flat[e, h] = t
 
         nc.sync.dma_start(offsets[:], offs)
         gate_col = keep.tile([P, PACK], F32, name="gate_col")
         nc.sync.dma_start(gate_col[:], gate[0].rearrange("(p j) -> p j", j=PACK))
+        make_identity(nc, ident[:])
         for q in range(4):
-            load_x_scales(q)
-        load_x()
-        load_wa(0)
+            rows = x_scales[0, 4 * q : 4 * q + 4, :].bitcast(I32)
+            nc.sync.dma_start(
+                xs_tab[32 * q : 32 * q + 32, :].bitcast(I32), rows.unsqueeze(0).to_broadcast([8, 4, T // 4])
+            )
+        nc.sync.dma_start(x_tab[:].bitcast(I32), x_words[0].rearrange("p t d -> p (t d)").bitcast(I32))
+        load_wa(0, 1)
         for q in range(4):
-            load_wa_scales(q)
-        load_wa(1)
-        load_wb_half(0, 0)
-        load_w_scales(0, 2)
-        load_wb_half(0, 1)
-        load_w(0, 1)
-        load_wb_half(1, 0)
-        load_wb_half(1, 1)
-        load_w(1, 2)
-        load_wa(2)
-        load_wb_half(2, 0)
-        load_wa(3)
-        load_wb_half(3, 0)
-        load_w_scales(2, 4)
-        load_w(2, 3)
-        last = keep.tile([P, P + 2 * PACK * HALF], F32, name="wb_last", align_bytes=64)
-        last_raw = last[:, P:].rearrange("p (e j n) -> p e j n", e=2, j=PACK)
-        for e in (2, 3):
-            nc.sync.dma_start(last_raw[:, e - 2], wb[e, :, HALF:].rearrange("(p j) n -> p j n", j=PACK))
-        load_w(3, 4)
+            nc.sync.dma_start(
+                wa_plane[32 * q : 32 * q + 16, :].bitcast(I32), wa_scales[:, 0, 4 * q : 4 * q + 4, :].bitcast(I32)
+            )
+        load_wa(1, 2)
+        load_wb(0, 0)
+        load_wa(2, 4)
+        load_w_scales(0)
+        load_w(0)
+        load_wb(1, 0)
+        load_w(1)
+        load_wb(2, 0)
+        load_w_scales(2)
+        load_w(2)
+        load_wb(3, 0)
+        load_w(3)
+        for e in range(E):
+            load_wb(e, 1)
 
-        xg, xgs, act, turned, hq, hqs, staged, wbq, wbqs = {}, {}, {}, {}, {}, {}, {}, {}, {}
+        hw = {}
+        xg, xgs, acts, staged, hq, hqs, wbq, wbqs = {}, {}, {}, {}, {}, {}, {}, {}
 
         def gather(e0, e1):
             lst = offsets[:, e0 * LIST_COLS : e1 * LIST_COLS]
@@ -138,8 +125,8 @@ def tile_moe_elr_gelu_kernel(
                 xg[e] = words[:, (e - e0) * C : (e - e0 + 1) * C].bitcast(FP8X4)
                 xgs[e] = scales[:, (e - e0) * C : (e - e0 + 1) * C]
 
-        def hidden(e, act_tag, pre_banks):
-            act[e] = keep.tile([P, H], BF16, name="act%d" % e, tag=act_tag, align_bytes=64)
+        def hidden(e, pre_banks):
+            act = keep.tile([P, H], BF16, name="act%d" % e, align_bytes=64)
             width = H // len(pre_banks)
             for a, bank in enumerate(pre_banks):
                 cols = slice(a * width, (a + 1) * width)
@@ -149,52 +136,46 @@ def tile_moe_elr_gelu_kernel(
                     rhs_scale=wa_plane[4 * e :, cols], start=True, stop=True,
                 )
                 nc.scalar.activation(
-                    act[e][:].rearrange("s (u p d) -> s u p d", u=2, d=2)[:, :, a * width // 4 : (a + 1) * width // 4, :],
+                    act[:].rearrange("s (u p d) -> s u p d", u=2, d=2)[:, :, a * width // 4 : (a + 1) * width // 4, :],
                     pre[:].rearrange("s (p u d) -> s u p d", u=2, d=2),
                     GELU,
                 )
+            acts[e] = act
 
         def turn(e, turned_bank):
-            turned[e] = psum.tile([P, 2, C], F32, name="turned%d" % e, tag="bank%d" % turned_bank)
-            pairs = act[e][:].bitcast(F32)
+            act = acts[e]
+            turned = psum.tile([P, 2, C], F32, name="turned%d" % e, tag="bank%d" % turned_bank)
+            pairs = act[:].bitcast(F32)
             for u in range(2):
-                nc.tensor.transpose(turned[e][:, u, :], pairs[:, u * P : (u + 1) * P], ident[:])
+                nc.tensor.transpose(turned[:, u, :], pairs[:, u * P : (u + 1) * P], ident[:])
+            words = keep.tile([P, 2 * C], F32, name="h%d" % e, tag="h%d" % e, align_bytes=64)
+            nc.scalar.copy(words[:].rearrange("p (s u) -> p s u", u=2), turned[:].rearrange("p u s -> p s u"))
+            hw[e] = words
 
-        def quantize_hidden(e, words):
-            nc.scalar.copy(words.rearrange("p (s u) -> p s u", u=2), turned[e][:].rearrange("p u s -> p s u"))
+        def quantize_h(e, tag):
             hq[e] = keep.tile([P, C], U32, name="hq%d" % e, align_bytes=64)
-            hqs[e] = keep.tile([P, C], U8, name="hqs%d" % e, align_bytes=64)
-            nc.vector.quantize_mx(out=hq[e][:].bitcast(FP8X4), scales=hqs[e][:], in_=words.bitcast(BF16))
+            hqs[e] = keep.tile([P, C], U8, name="hqs%d" % e, tag=tag, align_bytes=64)
+            nc.vector.quantize_mx(out=hq[e][:].bitcast(FP8X4), scales=hqs[e][:], in_=hw[e][:].bitcast(BF16))
 
-        def interleave(key, parts, copy, tag):
-            staged[key] = keep.tile([P, HALF * PACK], BF16, name="staged%s" % key, tag=tag, align_bytes=64)
-            at = 0
-            for part in parts:
-                width = part.shape[2]
-                copy(
-                    staged[key][:, at * PACK : (at + width) * PACK].rearrange("p (c i t) -> p c t i", i=4, t=PACK),
-                    part.rearrange("p t (c i) -> p c t i", i=4),
+        def interleave(e, h, tag):
+            staged[e, h] = keep.tile([P, HALF * PACK], BF16, name="staged%d_%d" % (e, h), tag=tag, align_bytes=64)
+            for m in range(2):
+                nc.vector.tensor_copy(
+                    staged[e, h][:, m * P * PACK : (m + 1) * P * PACK].rearrange("p (c i t) -> p c t i", i=4, t=PACK),
+                    raw[e, h][:, :, m * P : (m + 1) * P].rearrange("p t (c i) -> p c t i", i=4),
                 )
-                at = at + width
 
-        def interleave_pair(key, part, tag):
-            staged[key] = keep.tile([P, HALF * PACK], BF16, name="staged%s" % key, tag=tag, align_bytes=64)
-            nc.scalar.copy(
-                staged[key][:].rearrange("p (e c i t) -> p e c t i", e=2, i=4, t=PACK),
-                part.rearrange("p e t (c i) -> p e c t i", i=4),
-            )
+        def quantize_wb(e, h):
+            codes = keep.tile([P, HALF], U32, name="codes%d_%d" % (e, h), tag="codes%d_%d" % (e, h), align_bytes=64)
+            scales = keep.tile([P, HALF], U8, name="scales%d_%d" % (e, h), tag="scales%d_%d" % (e, h), align_bytes=64)
+            nc.vector.quantize_mx(out=codes[:].bitcast(FP8X4), scales=scales[:], in_=staged[e, h][:])
+            for m in range(2):
+                wbq[e, 2 * h + m] = codes[:, m * P : (m + 1) * P]
+                wbqs[e, 2 * h + m] = scales[:, m * P : (m + 1) * P]
 
-        def quantize_wb(key, blocks):
-            codes = keep.tile([P, HALF], U32, name="codes%s" % key, tag="codes%s" % key, align_bytes=64)
-            scales = keep.tile([P, HALF], U8, name="scales%s" % key, tag="scales%s" % key, align_bytes=64)
-            nc.vector.quantize_mx(out=codes[:].bitcast(FP8X4), scales=scales[:], in_=staged[key][:])
-            for m, eb in enumerate(blocks):
-                wbq[eb] = codes[:, m * P : (m + 1) * P]
-                wbqs[eb] = scales[:, m * P : (m + 1) * P]
-
-        def products(blocks, bank):
-            acc = psum.tile([P, len(blocks), C], F32, name="acc%d_%d" % blocks[0], tag="bank%d" % bank)
-            for m, (e, b) in enumerate(blocks):
+        def products(e, blocks, bank, home):
+            acc = psum.tile([P, len(blocks), C], F32, name="acc%d_%d" % (e, blocks[0]), tag="bank%d" % bank)
+            for m, b in enumerate(blocks):
                 n0 = b * P
                 nc.tensor.matmul_mx(
                     out=acc[:, m, :], lhsT=w_sb[e][:, 2 * n0 : 2 * (n0 + P)].bitcast(FP4X4),
@@ -204,94 +185,60 @@ def tile_moe_elr_gelu_kernel(
                     out=acc[:, m, :], lhsT=wbq[e, b].bitcast(FP8X4), lhsT_scale=wbqs[e, b],
                     rhs=hq[e][:].bitcast(FP8X4), rhs_scale=hqs[e][:], start=False, stop=True,
                 )
-            return acc
+            g = gates[:, e * C : (e + 1) * C].unsqueeze(1).to_broadcast([P, len(blocks), C])
+            nc.vector.tensor_tensor(home, acc[:], g, MULT)
 
-        def leave(acc, home):
-            nc.scalar.copy(home, acc[:].rearrange("p m s -> p (m s)"))
+        def window(b, e0, e1):
+            return windows[b][:].indirect(offsets[:, e0 * LIST_COLS : e1 * LIST_COLS])
 
-        def scatter(e0, e1, b, values, store):
-            t, c0 = gate_sb[e0]
-            nc.vector.tensor_tensor(
-                windows[b][:].indirect(offsets[:, e0 * LIST_COLS : e1 * LIST_COLS]),
-                values, t[:, c0 : c0 + (e1 - e0) * C], MULT,
-            )
-            if store:
-                nc.sync.dma_start(out[b * P : (b + 1) * P, :], windows[b][:])
+        def store(b):
+            nc.sync.dma_start(out[b * P : (b + 1) * P, :], windows[b][:])
 
-        def half_products(e, h, bank):
-            return products([(e, 2 * h), (e, 2 * h + 1)], bank)
-
-        def half_scatter(e, h, home, store):
-            for a in range(2):
-                scatter(e, e + 1, 2 * h + a, home[:, a * C : (a + 1) * C], store)
-
-        def fresh(name, width):
-            return keep.tile([P, width], F32, name=name, align_bytes=64)[:]
-
-        spread = psum.tile([P, PACK, P], F32, name="spread", tag="bank5")
+        spread = psum.tile([P, PACK, P], F32, name="spread", tag="bank7")
         for j in range(PACK):
             nc.tensor.transpose(spread[:, j, :], gate_col[:, j : j + 1].to_broadcast([P, P]), ident[:])
         gates = keep.tile([P, E * C], F32, name="gates")
         nc.scalar.copy(gates[:].rearrange("p (n j) -> p n j", j=PACK), spread[:].rearrange("p j n -> p n j"))
-        for e in range(E):
-            gate_sb[e] = (gates, e * C)
+
         gather(0, 1)
-        hidden(0, "act0", [0, 4])
-        turn(0, 1)
+        hidden(0, [0, 1])
         gather(1, 2)
-        hidden(1, "act1", [2])
-        turn(1, 7)
+        hidden(1, [3])
         gather(2, 4)
-        interleave("00", [raw[0, 0]], nc.vector.tensor_copy, "s00")
-        quantize_wb("00", [(0, 0), (0, 1)])
-        quantize_hidden(0, fresh("h0", 2 * C))
-        interleave("01", [raw[0, 1]], nc.vector.tensor_copy, "h0")
-        quantize_wb("01", [(0, 2), (0, 3)])
-        quantize_hidden(1, fresh("h1", 2 * C))
-        y0 = fresh("y0", C)
-        leave(products([(0, 0)], 5), y0)
-        scatter(0, 1, 0, y0, False)
-        y0b = fresh("y0b", C)
-        leave(products([(0, 1)], 6), y0b)
-        scatter(0, 1, 1, y0b, False)
-        interleave("10", [raw[1, 0]], nc.scalar.copy, "codes00")
-        quantize_wb("10", [(1, 0), (1, 1)])
-        y01 = flat[1, 0][:, :HALF]
-        leave(half_products(0, 1, 3), y01)
-        half_scatter(0, 1, y01, False)
-        interleave("11", [raw[1, 1][:, :, :64], raw[1, 1][:, :, 64:]], nc.scalar.copy, "s00")
-        quantize_wb("11", [(1, 2), (1, 3)])
-        y10 = fresh("y10", 2 * C)
-        leave(half_products(1, 0, 4), y10)
-        half_scatter(1, 0, y10, False)
-        hidden(2, "scales10", [0, 3])
-        interleave("20", [raw[2, 0]], nc.scalar.copy, "codes10")
-        quantize_wb("20", [(2, 0), (2, 1)])
-        acc11 = half_products(1, 1, 5)
-        turn(2, 1)
-        quantize_hidden(2, fresh("h2", 2 * C))
-        y11 = flat[2, 0][:, :HALF]
-        leave(acc11, y11)
-        half_scatter(1, 1, y11, False)
-        hidden(3, "scales11", [4])
-        interleave("30", [raw[3, 0]], nc.scalar.copy, "codes11")
-        quantize_wb("30", [(3, 0), (3, 1)])
-        acc20 = half_products(2, 0, 6)
-        turn(3, 2)
-        quantize_hidden(3, fresh("h3", 2 * C))
-        y20 = flat[3, 0][:, :HALF]
-        leave(acc20, y20)
-        half_scatter(2, 0, y20, False)
-        interleave_pair("b2", last_raw[:, :, :, :P], "codes20")
-        quantize_wb("b2", [(2, 2), (3, 2)])
-        y30 = last[:, : 2 * C]
-        leave(half_products(3, 0, 7), y30)
-        half_scatter(3, 0, y30, True)
-        interleave_pair("b3", last_raw[:, :, :, P:], "codes20")
-        quantize_wb("b3", [(2, 3), (3, 3)])
-        y2 = fresh("y2", 2 * C)
-        leave(products([(2, 2), (3, 2)], 0), y2)
-        scatter(2, 4, 2, y2, True)
-        y3 = fresh("y3", 2 * C)
-        leave(products([(2, 3), (3, 3)], 1), y3)
-        scatter(2, 4, 3, y3, True)
+        interleave(0, 0, "first")
+        quantize_wb(0, 0)
+        turn(0, 2)
+        quantize_h(0, "first")
+        turn(1, 4)
+        quantize_h(1, "hqs1")
+        interleave(1, 0, "h0")
+        y0 = raw[1, 0][:, 0:2, 0:C]
+        for b in range(2):
+            products(0, [b], (7, 3)[b], y0[:, b : b + 1, :])
+            nc.scalar.activation(window(b, 0, 1), y0[:, b, :], COPY)
+        hidden(2, [5])
+        hidden(3, [2])
+        turn(2, 7)
+        turn(3, 3)
+        units = [(e, h) for h in range(2) for e in range(E)]
+        last = raw[3, 1][:, 0:2, :]
+        quantize_wb(1, 0)
+        for u in range(1, len(units)):
+            e, h = units[u]
+            if u + 1 < len(units):
+                interleave(*units[u + 1], "codes%d_%d" % units[u - 1])
+            if u < 6:
+                y = raw[units[u + 1]][:, 0:2, 0:C]
+            else:
+                y = last[:, :, (e - 2) * C : (e - 1) * C]
+            if u in (2, 3):
+                quantize_h(u, "codes%d_0" % (u - 2))
+            products(e, [2 * h, 2 * h + 1], (6, 0, 1, 4, 5, 2, 6)[u - 1], y)
+            if u + 1 < len(units):
+                quantize_wb(*units[u + 1])
+            for m in (1, 0) if u < 6 else (0,):
+                nc.scalar.activation(window(2 * h + m, e, e + 1), y[:, m, :], COPY)
+                if e == E - 1:
+                    store(2 * h + m)
+        nc.vector.tensor_copy(window(3, 2, 4), last[:, 1, :])
+        store(3)

@@ -39,14 +39,11 @@ def tile_moe_elr_gelu_kernel(
         windows = [keep.tile([P, T], F32, name="window%d" % b) for b in range(N // P)]
         ident = keep.tile([P, P], F32, name="ident")
         zero = keep.tile([P, 8], F32, name="zero")
-        w_planes = {
-            e0: keep.tile([P, 2 * N], U8, name="w_plane%d" % e0, align_bytes=64) for e0 in (0, 2)
-        }
+        w_plane = keep.tile([P, E * N], U8, name="w_plane", align_bytes=64)
 
         nc.vector.memset(wa_plane[:].bitcast(I32), 0)
         nc.vector.memset(zero[:], 0.0)
-        for plane in w_planes.values():
-            nc.vector.memset(plane[:].bitcast(I32), 0)
+        nc.vector.memset(w_plane[:].bitcast(I32), 0)
         for b in range(2):
             nc.vector.memset(windows[b][:], 0.0)
         for b in range(2, 4):
@@ -54,14 +51,14 @@ def tile_moe_elr_gelu_kernel(
 
         wa_sb, w_sb, ws_sb, raw = {}, {}, {}, {}
 
-        def load_w_scales(e0):
+        def load_w_scales():
             for r in range(4):
                 nc.sync.dma_start(
-                    w_planes[e0][r:P:32, :].bitcast(I32).rearrange("q (e n) -> q e n", e=2),
-                    w_scales[e0 : e0 + 2, 0, r:16:4, :].rearrange("e q n -> q e n").bitcast(I32),
+                    w_plane[r:P:32, :].bitcast(I32).rearrange("q (e n) -> q e n", e=E),
+                    w_scales[:, 0, r:16:4, :].rearrange("e q n -> q e n").bitcast(I32),
                 )
-            for e in range(e0, e0 + 2):
-                ws_sb[e] = w_planes[e0][:, (e - e0) * N : (e - e0 + 1) * N]
+            for e in range(E):
+                ws_sb[e] = w_plane[:, e * N : (e + 1) * N]
 
         def load_wa(e0, e1):
             t = keep.tile([P, (e1 - e0) * H], U32, name="wa%d" % e0, align_bytes=64)
@@ -72,16 +69,26 @@ def tile_moe_elr_gelu_kernel(
             for e in range(e0, e1):
                 wa_sb[e] = t[:, (e - e0) * H : (e - e0 + 1) * H]
 
-        def load_w(e):
-            t = keep.tile([P, 2 * N], U8, name="w%d" % e, align_bytes=64)
-            nc.sync.dma_start(t[:].bitcast(I32), w_words[e, 0].bitcast(I32))
-            w_sb[e] = t[:]
+        def load_w(e0, e1):
+            t = keep.tile([P, (e1 - e0) * 2 * N], U8, name="w%d" % e0, align_bytes=64)
+            nc.sync.dma_start(
+                t[:].bitcast(I32).rearrange("p (e n) -> p e n", e=e1 - e0),
+                w_words[e0:e1, 0].rearrange("e p n -> p e n").bitcast(I32),
+            )
+            for e in range(e0, e1):
+                w_sb[e] = t[:, (e - e0) * 2 * N : (e - e0 + 1) * 2 * N]
 
-        def load_wb(e, h):
-            t = keep.tile([P, PACK * HALF], F32, name="wb%d_%d" % (e, h), align_bytes=64)
-            raw[e, h] = t[:].rearrange("p (j n) -> p j n", j=PACK)
+        def load_wb(e):
+            t = keep.tile([P, PACK * N], F32, name="wb%d" % e, align_bytes=64)
+            nc.sync.dma_start(t[:], wb[e].rearrange("(p j) n -> p (j n)", j=PACK))
+            for h in range(2):
+                raw[e, h] = t[:].rearrange("p (j n) -> p j n", j=PACK)[:, :, h * HALF : (h + 1) * HALF]
+
+        def load_wb_half(e, h):
+            raw[e, h] = rows_of[e][:].rearrange("p (j n) -> p j n", j=PACK)[:, :, h * HALF : (h + 1) * HALF]
             nc.sync.dma_start(raw[e, h], wb[e, :, h * HALF : (h + 1) * HALF].rearrange("(p j) n -> p j n", j=PACK))
 
+        rows_of = {e: keep.tile([P, PACK * N], F32, name="wb%d" % e, align_bytes=64) for e in (2, 3)}
         nc.sync.dma_start(offsets[:], offs)
         gate_col = keep.tile([P, PACK], F32, name="gate_col")
         nc.sync.dma_start(gate_col[:], gate[0].rearrange("(p j) -> p j", j=PACK))
@@ -98,19 +105,17 @@ def tile_moe_elr_gelu_kernel(
                 wa_plane[32 * q : 32 * q + 16, :].bitcast(I32), wa_scales[:, 0, 4 * q : 4 * q + 4, :].bitcast(I32)
             )
         load_wa(1, 2)
-        load_wb(0, 0)
+        load_wb(0)
         load_wa(2, 4)
-        load_w_scales(0)
-        load_w(0)
-        load_wb(1, 0)
-        load_w(1)
-        load_wb(2, 0)
-        load_w_scales(2)
-        load_w(2)
-        load_wb(3, 0)
-        load_w(3)
-        for e in range(E):
-            load_wb(e, 1)
+        load_w_scales()
+        load_w(0, 1)
+        load_wb(1)
+        load_w(1, 2)
+        load_wb_half(2, 0)
+        load_w(2, 4)
+        load_wb_half(3, 0)
+        load_wb_half(2, 1)
+        load_wb_half(3, 1)
 
         hw = {}
         xg, xgs, acts, staged, hq, hqs, wbq, wbqs = {}, {}, {}, {}, {}, {}, {}, {}
@@ -142,20 +147,24 @@ def tile_moe_elr_gelu_kernel(
                 )
             acts[e] = act
 
-        def turn(e, turned_bank):
-            act = acts[e]
-            turned = psum.tile([P, 2, C], F32, name="turned%d" % e, tag="bank%d" % turned_bank)
-            pairs = act[:].bitcast(F32)
-            for u in range(2):
-                nc.tensor.transpose(turned[:, u, :], pairs[:, u * P : (u + 1) * P], ident[:])
-            words = keep.tile([P, 2 * C], F32, name="h%d" % e, tag="h%d" % e, align_bytes=64)
-            nc.scalar.copy(words[:].rearrange("p (s u) -> p s u", u=2), turned[:].rearrange("p u s -> p s u"))
-            hw[e] = words
+        def turn(e0, e1, bank):
+            turned = psum.tile([P, e1 - e0, 2, C], F32, name="turned%d" % e0, tag="bank%d" % bank)
+            for e in range(e0, e1):
+                pairs = acts[e][:].bitcast(F32)
+                for u in range(2):
+                    nc.tensor.transpose(turned[:, e - e0, u, :], pairs[:, u * P : (u + 1) * P], ident[:])
+            hw[e0] = keep.tile([P, (e1 - e0) * 2 * C], F32, name="h%d" % e0, align_bytes=64)
+            nc.scalar.copy(
+                hw[e0][:].rearrange("p (e s u) -> p e s u", s=C, u=2), turned[:].rearrange("p e u s -> p e s u")
+            )
 
-        def quantize_h(e, tag):
-            hq[e] = keep.tile([P, C], U32, name="hq%d" % e, align_bytes=64)
-            hqs[e] = keep.tile([P, C], U8, name="hqs%d" % e, tag=tag, align_bytes=64)
-            nc.vector.quantize_mx(out=hq[e][:].bitcast(FP8X4), scales=hqs[e][:], in_=hw[e][:].bitcast(BF16))
+        def quantize_h(e0, e1, tag):
+            codes = keep.tile([P, (e1 - e0) * C], U32, name="hq%d" % e0, align_bytes=64)
+            scales = keep.tile([P, (e1 - e0) * C], U8, name="hqs%d" % e0, tag=tag, align_bytes=64)
+            nc.vector.quantize_mx(out=codes[:].bitcast(FP8X4), scales=scales[:], in_=hw[e0][:].bitcast(BF16))
+            for e in range(e0, e1):
+                hq[e] = codes[:, (e - e0) * C : (e - e0 + 1) * C]
+                hqs[e] = scales[:, (e - e0) * C : (e - e0 + 1) * C]
 
         def interleave(e, h, tag):
             staged[e, h] = keep.tile([P, HALF * PACK], BF16, name="staged%d_%d" % (e, h), tag=tag, align_bytes=64)
@@ -173,18 +182,23 @@ def tile_moe_elr_gelu_kernel(
                 wbq[e, 2 * h + m] = codes[:, m * P : (m + 1) * P]
                 wbqs[e, 2 * h + m] = scales[:, m * P : (m + 1) * P]
 
-        def products(e, blocks, bank, home):
+        def products(e, blocks, bank):
             acc = psum.tile([P, len(blocks), C], F32, name="acc%d_%d" % (e, blocks[0]), tag="bank%d" % bank)
             for m, b in enumerate(blocks):
-                n0 = b * P
                 nc.tensor.matmul_mx(
-                    out=acc[:, m, :], lhsT=w_sb[e][:, 2 * n0 : 2 * (n0 + P)].bitcast(FP4X4),
-                    lhsT_scale=ws_sb[e][:, n0 : n0 + P], rhs=xg[e], rhs_scale=xgs[e], start=True, stop=False,
+                    out=acc[:, m, :], lhsT=w_sb[e][:, 2 * b * P : 2 * (b + 1) * P].bitcast(FP4X4),
+                    lhsT_scale=ws_sb[e][:, b * P : (b + 1) * P], rhs=xg[e], rhs_scale=xgs[e],
+                    start=(m == 0), stop=False,
                 )
+            for m, b in enumerate(blocks):
                 nc.tensor.matmul_mx(
                     out=acc[:, m, :], lhsT=wbq[e, b].bitcast(FP8X4), lhsT_scale=wbqs[e, b],
-                    rhs=hq[e][:].bitcast(FP8X4), rhs_scale=hqs[e][:], start=False, stop=True,
+                    rhs=hq[e].bitcast(FP8X4), rhs_scale=hqs[e], start=False, stop=(m == len(blocks) - 1),
                 )
+            return acc
+
+        def leave(e, acc, home):
+            blocks = range(acc.shape[1])
             g = gates[:, e * C : (e + 1) * C].unsqueeze(1).to_broadcast([P, len(blocks), C])
             nc.vector.tensor_tensor(home, acc[:], g, MULT)
 
@@ -207,38 +221,51 @@ def tile_moe_elr_gelu_kernel(
         gather(2, 4)
         interleave(0, 0, "first")
         quantize_wb(0, 0)
-        turn(0, 2)
-        quantize_h(0, "first")
-        turn(1, 4)
-        quantize_h(1, "hqs1")
-        interleave(1, 0, "h0")
-        y0 = raw[1, 0][:, 0:2, 0:C]
-        for b in range(2):
-            products(0, [b], (7, 3)[b], y0[:, b : b + 1, :])
-            nc.scalar.activation(window(b, 0, 1), y0[:, b, :], COPY)
-        hidden(2, [5])
+        turn(0, 1, 2)
+        quantize_h(0, 1, "first")
+        turn(1, 2, 4)
+        interleave(0, 1, "second")
+        hidden(2, [0])
         hidden(3, [2])
-        turn(2, 7)
-        turn(3, 3)
-        units = [(e, h) for h in range(2) for e in range(E)]
-        last = raw[3, 1][:, 0:2, :]
-        quantize_wb(1, 0)
-        for u in range(1, len(units)):
+        y0 = keep.tile([P, 4, C], F32, name="y0")
+        for b in range(2):
+            leave(0, products(0, [b], (7, 5)[b]), y0[:, b : b + 1, :])
+        nc.scalar.activation(window(0, 0, 1), y0[:, 0, :], COPY)
+        quantize_wb(0, 1)
+        quantize_h(1, 2, "second")
+        leave(0, products(0, [2, 3], 6), y0[:, 2:4, :])
+        turn(2, 4, 7)
+        nc.vector.tensor_copy(window(1, 0, 1), y0[:, 1, :])
+        for b in (3, 2):
+            nc.scalar.activation(window(b, 0, 1), y0[:, b, :], COPY)
+        units = [(0, 0), (0, 1), (1, 0), (1, 1), (2, 0), (3, 0), (2, 1), (3, 1)]
+        banks = (None, None, 1, 3, 4, 1, 3, 4)
+        for u in (2, 3):
+            interleave(*units[u], "codes%d_%d" % units[u - 2])
+            quantize_wb(*units[u])
+        quantize_h(2, 4, "codes0_0")
+        homes = {
+            2: raw[2, 0][:, 0:2, :C],
+            3: raw[3, 0][:, 0:2, :C],
+            4: raw[2, 1][:, 0:2, :C],
+            5: raw[3, 1][:, 2:4, :C],
+            6: rows_of[3][:, HALF : HALF + 2 * (N - C)].rearrange("p (m x) -> p m x", m=2)[:, :, :C],
+            7: raw[3, 1][:, 0:2, C:],
+        }
+        for u in range(2, len(units)):
             e, h = units[u]
-            if u + 1 < len(units):
-                interleave(*units[u + 1], "codes%d_%d" % units[u - 1])
-            if u < 6:
-                y = raw[units[u + 1]][:, 0:2, 0:C]
-            else:
-                y = last[:, :, (e - 2) * C : (e - 1) * C]
-            if u in (2, 3):
-                quantize_h(u, "codes%d_0" % (u - 2))
-            products(e, [2 * h, 2 * h + 1], (6, 0, 1, 4, 5, 2, 6)[u - 1], y)
-            if u + 1 < len(units):
-                quantize_wb(*units[u + 1])
-            for m in (1, 0) if u < 6 else (0,):
-                nc.scalar.activation(window(2 * h + m, e, e + 1), y[:, m, :], COPY)
+            acc = products(e, [2 * h, 2 * h + 1], banks[u])
+            if u + 2 < len(units):
+                interleave(*units[u + 2], "codes%d_%d" % units[u])
+            leave(e, acc, homes[u])
+            if u + 2 < len(units):
+                quantize_wb(*units[u + 2])
+            if u == 6:
+                nc.vector.tensor_copy(window(3, 1, 3), raw[3, 0][:, 1, :])
+            if u == 7:
+                nc.vector.tensor_copy(window(3, 3, 4), homes[u][:, 1, :])
+            for m in (0,) if h == 1 else (1, 0):
+                nc.scalar.activation(window(2 * h + m, e, e + 1), homes[u][:, m, :], COPY)
                 if e == E - 1:
                     store(2 * h + m)
-        nc.vector.tensor_copy(window(3, 2, 4), last[:, 1, :])
         store(3)

@@ -39,11 +39,12 @@ def tile_moe_elr_gelu_kernel(
         windows = [keep.tile([P, T], F32, name="window%d" % b) for b in range(N // P)]
         ident = keep.tile([P, P], F32, name="ident")
         zero = keep.tile([P, 8], F32, name="zero")
-        w_plane = keep.tile([P, E * N], U8, name="w_plane", align_bytes=64)
+        w_planes = {e0: keep.tile([P, 2 * N], U8, name="w_plane%d" % e0, align_bytes=64) for e0 in (0, 2)}
 
         nc.vector.memset(wa_plane[:].bitcast(I32), 0)
         nc.vector.memset(zero[:], 0.0)
-        nc.vector.memset(w_plane[:].bitcast(I32), 0)
+        for plane in w_planes.values():
+            nc.vector.memset(plane[:].bitcast(I32), 0)
         for b in range(2):
             nc.vector.memset(windows[b][:], 0.0)
         for b in range(2, 4):
@@ -51,14 +52,14 @@ def tile_moe_elr_gelu_kernel(
 
         wa_sb, w_sb, ws_sb, raw = {}, {}, {}, {}
 
-        def load_w_scales():
+        def load_w_scales(e0):
             for r in range(4):
                 nc.sync.dma_start(
-                    w_plane[r:P:32, :].bitcast(I32).rearrange("q (e n) -> q e n", e=E),
-                    w_scales[:, 0, r:16:4, :].rearrange("e q n -> q e n").bitcast(I32),
+                    w_planes[e0][r:P:32, :].bitcast(I32).rearrange("q (e n) -> q e n", e=2),
+                    w_scales[e0 : e0 + 2, 0, r:16:4, :].rearrange("e q n -> q e n").bitcast(I32),
                 )
-            for e in range(E):
-                ws_sb[e] = w_plane[:, e * N : (e + 1) * N]
+            for e in range(e0, e0 + 2):
+                ws_sb[e] = w_planes[e0][:, (e - e0) * N : (e - e0 + 1) * N]
 
         def load_wa(e0, e1):
             t = keep.tile([P, (e1 - e0) * H], U32, name="wa%d" % e0, align_bytes=64)
@@ -91,7 +92,6 @@ def tile_moe_elr_gelu_kernel(
         rows_of = {e: keep.tile([P, PACK * N], F32, name="wb%d" % e, align_bytes=64) for e in (2, 3)}
         nc.sync.dma_start(offsets[:], offs)
         gate_col = keep.tile([P, PACK], F32, name="gate_col")
-        nc.sync.dma_start(gate_col[:], gate[0].rearrange("(p j) -> p j", j=PACK))
         make_identity(nc, ident[:])
         for q in range(4):
             rows = x_scales[0, 4 * q : 4 * q + 4, :].bitcast(I32)
@@ -100,20 +100,22 @@ def tile_moe_elr_gelu_kernel(
             )
         nc.sync.dma_start(x_tab[:].bitcast(I32), x_words[0].rearrange("p t d -> p (t d)").bitcast(I32))
         load_wa(0, 1)
+        load_wa(1, 2)
         for q in range(4):
             nc.sync.dma_start(
                 wa_plane[32 * q : 32 * q + 16, :].bitcast(I32), wa_scales[:, 0, 4 * q : 4 * q + 4, :].bitcast(I32)
             )
-        load_wa(1, 2)
         load_wb(0)
+        nc.sync.dma_start(gate_col[:], gate[0].rearrange("(p j) -> p j", j=PACK))
         load_wa(2, 4)
-        load_w_scales()
+        load_w_scales(0)
         load_w(0, 1)
         load_wb(1)
         load_w(1, 2)
         load_wb_half(2, 0)
-        load_w(2, 4)
         load_wb_half(3, 0)
+        load_w_scales(2)
+        load_w(2, 4)
         load_wb_half(2, 1)
         load_wb_half(3, 1)
 
@@ -245,27 +247,41 @@ def tile_moe_elr_gelu_kernel(
             quantize_wb(*units[u])
         quantize_h(2, 4, "codes0_0")
         homes = {
-            2: raw[2, 0][:, 0:2, :C],
+            2: keep.tile([P, 2, C], F32, name="y2", align_bytes=64)[:],
             3: raw[3, 0][:, 0:2, :C],
-            4: raw[2, 1][:, 0:2, :C],
-            5: raw[3, 1][:, 2:4, :C],
-            6: rows_of[3][:, HALF : HALF + 2 * (N - C)].rearrange("p (m x) -> p m x", m=2)[:, :, :C],
+            6: raw[3, 1][:, 0:2, :C],
             7: raw[3, 1][:, 0:2, C:],
         }
-        for u in range(2, len(units)):
+
+        def finish(u, acc):
             e, h = units[u]
-            acc = products(e, [2 * h, 2 * h + 1], banks[u])
-            if u + 2 < len(units):
-                interleave(*units[u + 2], "codes%d_%d" % units[u])
             leave(e, acc, homes[u])
-            if u + 2 < len(units):
-                quantize_wb(*units[u + 2])
-            if u == 6:
-                nc.vector.tensor_copy(window(3, 1, 3), raw[3, 0][:, 1, :])
-            if u == 7:
-                nc.vector.tensor_copy(window(3, 3, 4), homes[u][:, 1, :])
             for m in (0,) if h == 1 else (1, 0):
                 nc.scalar.activation(window(2 * h + m, e, e + 1), homes[u][:, m, :], COPY)
-                if e == E - 1:
-                    store(2 * h + m)
+
+        def multiply(u):
+            e, h = units[u]
+            return products(e, [2 * h, 2 * h + 1], banks[u])
+
+        for u in (2, 3):
+            acc = multiply(u)
+            interleave(*units[u + 2], "codes%d_%d" % units[u])
+            finish(u, acc)
+            quantize_wb(*units[u + 2])
+        homes[4] = raw[3, 0][:, 2:4, :C]
+        finish(4, multiply(4))
+        nc.vector.tensor_copy(window(3, 1, 2), homes[3][:, 1, :])
+        interleave(*units[6], "codes2_0")
+        homes[5] = raw[2, 1][:, 0:2, :C]
+        finish(5, multiply(5))
+        quantize_wb(*units[6])
+        interleave(*units[7], "codes3_0")
+        quantize_wb(*units[7])
+        store(1)
+        store(0)
+        finish(6, multiply(6))
+        nc.vector.tensor_copy(window(3, 2, 3), homes[6][:, 1, :])
+        finish(7, multiply(7))
+        nc.vector.tensor_copy(window(3, 3, 4), homes[7][:, 1, :])
         store(3)
+        store(2)

@@ -99,14 +99,13 @@ def tile_moe_elr_gelu_kernel(
                 xs_tab[32 * q : 32 * q + 32, :].bitcast(I32), rows.unsqueeze(0).to_broadcast([8, 4, T // 4])
             )
         nc.sync.dma_start(x_tab[:].bitcast(I32), x_words[0].rearrange("p t d -> p (t d)").bitcast(I32))
-        load_wa(0, 1)
-        load_wa(1, 2)
+        load_wa(0, 2)
         for q in range(4):
             nc.sync.dma_start(
                 wa_plane[32 * q : 32 * q + 16, :].bitcast(I32), wa_scales[:, 0, 4 * q : 4 * q + 4, :].bitcast(I32)
             )
-        load_wb(0)
         nc.sync.dma_start(gate_col[:], gate[0].rearrange("(p j) -> p j", j=PACK))
+        load_wb(0)
         load_wa(2, 4)
         load_w_scales(0)
         load_w(0, 1)
@@ -168,10 +167,10 @@ def tile_moe_elr_gelu_kernel(
                 hq[e] = codes[:, (e - e0) * C : (e - e0 + 1) * C]
                 hqs[e] = scales[:, (e - e0) * C : (e - e0 + 1) * C]
 
-        def interleave(e, h, tag):
+        def interleave(e, h, tag, first=nc.vector.tensor_copy):
             staged[e, h] = keep.tile([P, HALF * PACK], BF16, name="staged%d_%d" % (e, h), tag=tag, align_bytes=64)
-            for m in range(2):
-                nc.vector.tensor_copy(
+            for m, copy in enumerate((first, nc.vector.tensor_copy)):
+                copy(
                     staged[e, h][:, m * P * PACK : (m + 1) * P * PACK].rearrange("p (c i t) -> p c t i", i=4, t=PACK),
                     raw[e, h][:, :, m * P : (m + 1) * P].rearrange("p t (c i) -> p c t i", i=4),
                 )
@@ -265,7 +264,7 @@ def tile_moe_elr_gelu_kernel(
 
         for u in (2, 3):
             acc = multiply(u)
-            interleave(*units[u + 2], "codes%d_%d" % units[u])
+            interleave(*units[u + 2], "codes%d_%d" % units[u], (nc.scalar.copy, nc.vector.tensor_copy)[u - 2])
             finish(u, acc)
             quantize_wb(*units[u + 2])
         homes[4] = raw[3, 0][:, 2:4, :C]

@@ -196,12 +196,12 @@ def tile_moe_elr_gelu_kernel(
                     out=acc[:, m, :], lhsT=wbq[e, b].bitcast(FP8X4), lhsT_scale=wbqs[e, b],
                     rhs=hq[e].bitcast(FP8X4), rhs_scale=hqs[e], start=False, stop=(m == len(blocks) - 1),
                 )
-            return acc
+            return acc[:]
 
         def leave(e, acc, home):
             blocks = range(acc.shape[1])
             g = gates[:, e * C : (e + 1) * C].unsqueeze(1).to_broadcast([P, len(blocks), C])
-            nc.vector.tensor_tensor(home, acc[:], g, MULT)
+            nc.vector.tensor_tensor(home, acc, g, MULT)
 
         def window(b, e0, e1):
             return windows[b][:].indirect(offsets[:, e0 * LIST_COLS : e1 * LIST_COLS])
@@ -240,7 +240,7 @@ def tile_moe_elr_gelu_kernel(
         for b in (3, 2):
             nc.scalar.activation(window(b, 0, 1), y0[:, b, :], COPY)
         units = [(0, 0), (0, 1), (1, 0), (1, 1), (2, 0), (3, 0), (2, 1), (3, 1)]
-        banks = (None, None, 1, 3, 4, 1, 3, 4)
+        banks = (None, None, 1, 3, 4, 1, 4, 3)
         for u in (2, 3):
             interleave(*units[u], "codes%d_%d" % units[u - 2])
             quantize_wb(*units[u])
@@ -262,18 +262,24 @@ def tile_moe_elr_gelu_kernel(
             e, h = units[u]
             return products(e, [2 * h, 2 * h + 1], banks[u])
 
-        for u in (2, 3):
-            acc = multiply(u)
-            interleave(*units[u + 2], "codes%d_%d" % units[u], (nc.scalar.copy, nc.vector.tensor_copy)[u - 2])
-            finish(u, acc)
-            quantize_wb(*units[u + 2])
+        acc = multiply(2)
+        interleave(*units[4], "codes1_0", nc.scalar.copy)
+        finish(2, acc)
+        quantize_wb(*units[4])
+        acc3 = multiply(3)
+        interleave(*units[5], "codes1_1")
+        leave(1, acc3[:, 0:1, :], homes[3][:, 0:1, :])
+        nc.scalar.activation(window(2, 1, 2), homes[3][:, 0, :], COPY)
+        quantize_wb(*units[5])
         homes[4] = raw[3, 0][:, 2:4, :C]
         finish(4, multiply(4))
-        nc.vector.tensor_copy(window(3, 1, 2), homes[3][:, 1, :])
         interleave(*units[6], "codes2_0")
+        late = raw[2, 1][:, 2:3, :C]
+        leave(1, acc3[:, 1:2, :], late)
         homes[5] = raw[2, 1][:, 0:2, :C]
         finish(5, multiply(5))
         quantize_wb(*units[6])
+        nc.vector.tensor_copy(window(3, 1, 2), late[:, 0, :])
         interleave(*units[7], "codes3_0")
         quantize_wb(*units[7])
         store(1)

@@ -99,13 +99,14 @@ def tile_moe_elr_gelu_kernel(
                 xs_tab[32 * q : 32 * q + 32, :].bitcast(I32), rows.unsqueeze(0).to_broadcast([8, 4, T // 4])
             )
         nc.sync.dma_start(x_tab[:].bitcast(I32), x_words[0].rearrange("p t d -> p (t d)").bitcast(I32))
-        load_wa(0, 2)
+        load_wa(0, 1)
+        load_wa(1, 2)
         for q in range(4):
             nc.sync.dma_start(
                 wa_plane[32 * q : 32 * q + 16, :].bitcast(I32), wa_scales[:, 0, 4 * q : 4 * q + 4, :].bitcast(I32)
             )
-        nc.sync.dma_start(gate_col[:], gate[0].rearrange("(p j) -> p j", j=PACK))
         load_wb(0)
+        nc.sync.dma_start(gate_col[:], gate[0].rearrange("(p j) -> p j", j=PACK))
         load_wa(2, 4)
         load_w_scales(0)
         load_w(0, 1)

@@ -149,6 +149,28 @@ def tile_moe_elr_gelu_kernel(
                 )
             acts[e] = act
 
+        def first_hidden(bank):
+            words = keep.tile([P, H], U32, name="wa_turned", align_bytes=64)
+            nc.scalar.copy(
+                words[:].rearrange("p (t c i) -> p c t i", t=PACK, i=4),
+                wa_sb[0].rearrange("p (c i t) -> p c t i", t=PACK, i=4),
+            )
+            plane = keep.tile([P, H], U8, name="wa_plane_turned", align_bytes=64)
+            nc.vector.tensor_copy(
+                plane[:].rearrange("p (t m) -> p m t", t=PACK), wa_plane[:].rearrange("p (m t) -> p m t", t=PACK)
+            )
+            pre = psum.tile([P, PACK, C], F32, name="pre0", tag="bank%d" % bank)
+            for t in range(PACK):
+                cols = slice(t * P, (t + 1) * P)
+                nc.tensor.matmul_mx(
+                    out=pre[:, t, :], lhsT=words[:, cols].bitcast(FP8X4), lhsT_scale=plane[:, cols],
+                    rhs=xg[0], rhs_scale=xgs[0], start=True, stop=True,
+                )
+            hw[0] = keep.tile([P, 2 * C], F32, name="h0", tag="h0", align_bytes=64)
+            nc.scalar.activation(
+                hw[0][:].bitcast(BF16).rearrange("p (s t) -> p s t", t=PACK), pre[:].rearrange("p t s -> p s t"), GELU
+            )
+
         def turn(e0, e1, bank):
             turned = psum.tile([P, e1 - e0, 2, C], F32, name="turned%d" % e0, tag="bank%d" % bank)
             for e in range(e0, e1):
@@ -176,9 +198,9 @@ def tile_moe_elr_gelu_kernel(
                     raw[e, h][:, :, m * P : (m + 1) * P].rearrange("p t (c i) -> p c t i", i=4),
                 )
 
-        def quantize_wb(e, h):
+        def quantize_wb(e, h, tag=None):
             codes = keep.tile([P, HALF], U32, name="codes%d_%d" % (e, h), tag="codes%d_%d" % (e, h), align_bytes=64)
-            scales = keep.tile([P, HALF], U8, name="scales%d_%d" % (e, h), tag="scales%d_%d" % (e, h), align_bytes=64)
+            scales = keep.tile([P, HALF], U8, name="scales%d_%d" % (e, h), tag=tag or "scales%d_%d" % (e, h), align_bytes=64)
             nc.vector.quantize_mx(out=codes[:].bitcast(FP8X4), scales=scales[:], in_=staged[e, h][:])
             for m in range(2):
                 wbq[e, 2 * h + m] = codes[:, m * P : (m + 1) * P]
@@ -217,23 +239,22 @@ def tile_moe_elr_gelu_kernel(
         nc.scalar.copy(gates[:].rearrange("p (n j) -> p n j", j=PACK), spread[:].rearrange("p j n -> p n j"))
 
         gather(0, 1)
-        hidden(0, [0, 1])
+        first_hidden(0)
         gather(1, 2)
         hidden(1, [3])
         gather(2, 4)
         interleave(0, 0, "first")
         quantize_wb(0, 0)
-        turn(0, 1, 2)
         quantize_h(0, 1, "first")
         turn(1, 2, 4)
         interleave(0, 1, "second")
-        hidden(2, [0])
+        hidden(2, [1])
         hidden(3, [2])
         y0 = keep.tile([P, 4, C], F32, name="y0")
         for b in range(2):
             leave(0, products(0, [b], (7, 5)[b]), y0[:, b : b + 1, :])
         nc.scalar.activation(window(0, 0, 1), y0[:, 0, :], COPY)
-        quantize_wb(0, 1)
+        quantize_wb(0, 1, "h0")
         quantize_h(1, 2, "second")
         leave(0, products(0, [2, 3], 6), y0[:, 2:4, :])
         turn(2, 4, 7)

@@ -41,6 +41,7 @@ def tile_moe_elr_gelu_kernel(
         zero = keep.tile([P, 8], F32, name="zero")
         w_planes = {e0: keep.tile([P, 2 * N], U8, name="w_plane%d" % e0, align_bytes=64) for e0 in (0, 2)}
 
+        nc.gpsimd.memset(xs_tab[:].bitcast(I32), 0)
         nc.vector.memset(wa_plane[:].bitcast(I32), 0)
         nc.vector.memset(zero[:], 0.0)
         for plane in w_planes.values():
@@ -93,11 +94,8 @@ def tile_moe_elr_gelu_kernel(
         nc.sync.dma_start(offsets[:], offs)
         gate_col = keep.tile([P, PACK], F32, name="gate_col")
         make_identity(nc, ident[:])
-        for q in range(4):
-            rows = x_scales[0, 4 * q : 4 * q + 4, :].bitcast(I32)
-            nc.sync.dma_start(
-                xs_tab[32 * q : 32 * q + 32, :].bitcast(I32), rows.unsqueeze(0).to_broadcast([8, 4, T // 4])
-            )
+        for r in range(4):
+            nc.sync.dma_start(xs_tab[r:P:32, :].bitcast(I32), x_scales[0, r:16:4, :].bitcast(I32))
         nc.sync.dma_start(x_tab[:].bitcast(I32), x_words[0].rearrange("p t d -> p (t d)").bitcast(I32))
         load_wa(0, 1)
         load_wa(1, 2)

@@ -94,10 +94,10 @@ def tile_moe_elr_gelu_kernel(
         nc.sync.dma_start(offsets[:], offs)
         gate_col = keep.tile([P, PACK], F32, name="gate_col")
         make_identity(nc, ident[:])
+        load_wa(0, 1)
         for r in range(4):
             nc.sync.dma_start(xs_tab[r:P:32, :].bitcast(I32), x_scales[0, r:16:4, :].bitcast(I32))
         nc.sync.dma_start(x_tab[:].bitcast(I32), x_words[0].rearrange("p t d -> p (t d)").bitcast(I32))
-        load_wa(0, 1)
         load_wa(1, 2)
         for q in range(4):
             nc.sync.dma_start(

from contextlib import ExitStack

import concourse.mybir as mybir
from concourse.masks import make_identity

K, T, E, C, H, N = 512, 1024, 4, 128, 512, 512
FLOPS = 2 * E * C * (K * H + K * N + H * N)

F32 = mybir.dt.float32
BF16 = mybir.dt.bfloat16
I32 = mybir.dt.int32
U32 = mybir.dt.uint32
U16 = mybir.dt.uint16
U8 = mybir.dt.uint8
FP8X4 = mybir.dt.float8_e4m3fn_x4
FP4X4 = mybir.dt.float4_e2m1fn_x4
GELU = mybir.ActivationFunctionType.Gelu_apprx_tanh
COPY = mybir.ActivationFunctionType.Copy
MULT = mybir.AluOpType.mult

P = 128
PACK = 4
HALF = N // 2
LIST_COLS = C // 16


def tile_moe_elr_gelu_kernel(
    tc, x_words, x_scales, w_words, w_scales, wa_words, wa_scales, wb, gate, offs, out
):
    nc = tc.nc
    with ExitStack() as ctx:
        keep = ctx.enter_context(tc.tile_pool(name="keep", bufs=1))
        psum = ctx.enter_context(tc.psum_pool(name="psum", bufs=1))

        offsets = keep.tile([P, E * LIST_COLS], U16, name="offsets")
        x_tab = keep.tile([P, T], U32, name="x_tab", align_bytes=64)
        xs_tab = keep.tile([P, T], U8, name="xs_tab", align_bytes=64)
        wa_plane = keep.tile([P, H], U8, name="wa_plane", align_bytes=64)
        windows = [keep.tile([P, T], F32, name="window%d" % b) for b in range(N // P)]
        ident = keep.tile([P, P], F32, name="ident")
        zero = keep.tile([P, 8], F32, name="zero")
        w_planes = {e0: keep.tile([P, 2 * N], U8, name="w_plane%d" % e0, align_bytes=64) for e0 in (0, 2)}

        nc.gpsimd.memset(xs_tab[:].bitcast(I32), 0)
        nc.vector.memset(wa_plane[:].bitcast(I32), 0)
        nc.vector.memset(zero[:], 0.0)
        for plane in w_planes.values():
            nc.vector.memset(plane[:].bitcast(I32), 0)
        for b in range(2):
            nc.vector.memset(windows[b][:], 0.0)
        for b in range(2, 4):
            nc.scalar.activation(windows[b][:], zero[:, 0:1].to_broadcast([P, T]), GELU)

        wa_sb, w_sb, ws_sb, raw = {}, {}, {}, {}

        def load_w_scales(e0):
            for r in range(4):
                nc.sync.dma_start(
                    w_planes[e0][r:P:32, :].bitcast(I32).rearrange("q (e n) -> q e n", e=2),
                    w_scales[e0 : e0 + 2, 0, r:16:4, :].rearrange("e q n -> q e n").bitcast(I32),
                )
            for e in range(e0, e0 + 2):
                ws_sb[e] = w_planes[e0][:, (e - e0) * N : (e - e0 + 1) * N]

        def load_wa(e0, e1):
            t = keep.tile([P, (e1 - e0) * H], U32, name="wa%d" % e0, align_bytes=64)
            nc.sync.dma_start(
                t[:].bitcast(I32).rearrange("p (e i) -> p e i", e=e1 - e0),
                wa_words[e0:e1, 0].rearrange("e p i d -> p e (i d)").bitcast(I32),
            )
            for e in range(e0, e1):
                wa_sb[e] = t[:, (e - e0) * H : (e - e0 + 1) * H]

        def load_w(e0, e1):
            t = keep.tile([P, (e1 - e0) * 2 * N], U8, name="w%d" % e0, align_bytes=64)
            nc.sync.dma_start(
                t[:].bitcast(I32).rearrange("p (e n) -> p e n", e=e1 - e0),
                w_words[e0:e1, 0].rearrange("e p n -> p e n").bitcast(I32),
            )
            for e in range(e0, e1):
                w_sb[e] = t[:, (e - e0) * 2 * N : (e - e0 + 1) * 2 * N]

        def load_wb(e):
            t = keep.tile([P, PACK * N], F32, name="wb%d" % e, align_bytes=64)
            nc.sync.dma_start(t[:], wb[e].rearrange("(p j) n -> p (j n)", j=PACK))
            for h in range(2):
                raw[e, h] = t[:].rearrange("p (j n) -> p j n", j=PACK)[:, :, h * HALF : (h + 1) * HALF]

        def load_wb_half(e, h):
            raw[e, h] = rows_of[e][:].rearrange("p (j n) -> p j n", j=PACK)[:, :, h * HALF : (h + 1) * HALF]
            nc.sync.dma_start(raw[e, h], wb[e, :, h * HALF : (h + 1) * HALF].rearrange("(p j) n -> p j n", j=PACK))

        rows_of = {e: keep.tile([P, PACK * N], F32, name="wb%d" % e, align_bytes=64) for e in (2, 3)}
        nc.sync.dma_start(offsets[:], offs)
        gate_col = keep.tile([P, PACK], F32, name="gate_col")
        make_identity(nc, ident[:])
        load_wa(0, 1)
        for r in range(4):
            nc.sync.dma_start(xs_tab[r:P:32, :].bitcast(I32), x_scales[0, r:16:4, :].bitcast(I32))
        nc.sync.dma_start(x_tab[:].bitcast(I32), x_words[0].rearrange("p t d -> p (t d)").bitcast(I32))
        load_wa(1, 2)
        for q in range(4):
            nc.sync.dma_start(
                wa_plane[32 * q : 32 * q + 16, :].bitcast(I32), wa_scales[:, 0, 4 * q : 4 * q + 4, :].bitcast(I32)
            )
        load_wb(0)
        nc.sync.dma_start(gate_col[:], gate[0].rearrange("(p j) -> p j", j=PACK))
        load_wa(2, 4)
        load_w_scales(0)
        load_w(0, 1)
        load_wb(1)
        load_w(1, 2)
        load_wb_half(2, 0)
        load_wb_half(3, 0)
        load_w_scales(2)
        load_w(2, 4)
        load_wb_half(2, 1)
        load_wb_half(3, 1)

        hw = {}
        xg, xgs, acts, staged, hq, hqs, wbq, wbqs = {}, {}, {}, {}, {}, {}, {}, {}

        def gather(e0, e1):
            lst = offsets[:, e0 * LIST_COLS : e1 * LIST_COLS]
            words = keep.tile([P, (e1 - e0) * C], U32, name="xg%d" % e0, align_bytes=64)
            scales = keep.tile([P, (e1 - e0) * C], U8, name="xgs%d" % e0, align_bytes=64)
            nc.vector.tensor_copy(words[:], x_tab[:].indirect(lst))
            nc.vector.tensor_copy(scales[:], xs_tab[:].indirect(lst))
            for e in range(e0, e1):
                xg[e] = words[:, (e - e0) * C : (e - e0 + 1) * C].bitcast(FP8X4)
                xgs[e] = scales[:, (e - e0) * C : (e - e0 + 1) * C]

        def hidden(e, pre_banks):
            act = keep.tile([P, H], BF16, name="act%d" % e, align_bytes=64)
            width = H // len(pre_banks)
            for a, bank in enumerate(pre_banks):
                cols = slice(a * width, (a + 1) * width)
                pre = psum.tile([P, width], F32, name="pre%d_%d" % (e, a), tag="bank%d" % bank)
                nc.tensor.matmul_mx(
                    out=pre[:], lhsT=xg[e], lhsT_scale=xgs[e], rhs=wa_sb[e][:, cols].bitcast(FP8X4),
                    rhs_scale=wa_plane[4 * e :, cols], start=True, stop=True,
                )
                nc.scalar.activation(
                    act[:].rearrange("s (u p d) -> s u p d", u=2, d=2)[:, :, a * width // 4 : (a + 1) * width // 4, :],
                    pre[:].rearrange("s (p u d) -> s u p d", u=2, d=2),
                    GELU,
                )
            acts[e] = act

        def first_hidden(bank):
            words = keep.tile([P, H], U32, name="wa_turned", align_bytes=64)
            nc.scalar.copy(
                words[:].rearrange("p (t c i) -> p c t i", t=PACK, i=4),
                wa_sb[0].rearrange("p (c i t) -> p c t i", t=PACK, i=4),
            )
            plane = keep.tile([P, H], U8, name="wa_plane_turned", align_bytes=64)
            nc.vector.tensor_copy(
                plane[:].rearrange("p (t m) -> p m t", t=PACK), wa_plane[:].rearrange("p (m t) -> p m t", t=PACK)
            )
            pre = psum.tile([P, PACK, C], F32, name="pre0", tag="bank%d" % bank)
            for t in range(PACK):
                cols = slice(t * P, (t + 1) * P)
                nc.tensor.matmul_mx(
                    out=pre[:, t, :], lhsT=words[:, cols].bitcast(FP8X4), lhsT_scale=plane[:, cols],
                    rhs=xg[0], rhs_scale=xgs[0], start=True, stop=True,
                )
            hw[0] = keep.tile([P, 2 * C], F32, name="h0", tag="h0", align_bytes=64)
            nc.scalar.activation(
                hw[0][:].bitcast(BF16).rearrange("p (s t) -> p s t", t=PACK), pre[:].rearrange("p t s -> p s t"), GELU
            )

        def turn(e0, e1, bank):
            turned = psum.tile([P, e1 - e0, 2, C], F32, name="turned%d" % e0, tag="bank%d" % bank)
            for e in range(e0, e1):
                pairs = acts[e][:].bitcast(F32)
                for u in range(2):
                    nc.tensor.transpose(turned[:, e - e0, u, :], pairs[:, u * P : (u + 1) * P], ident[:])
            hw[e0] = keep.tile([P, (e1 - e0) * 2 * C], F32, name="h%d" % e0, align_bytes=64)
            nc.scalar.copy(
                hw[e0][:].rearrange("p (e s u) -> p e s u", s=C, u=2), turned[:].rearrange("p e u s -> p e s u")
            )

        def quantize_h(e0, e1, tag):
            codes = keep.tile([P, (e1 - e0) * C], U32, name="hq%d" % e0, align_bytes=64)
            scales = keep.tile([P, (e1 - e0) * C], U8, name="hqs%d" % e0, tag=tag, align_bytes=64)
            nc.vector.quantize_mx(out=codes[:].bitcast(FP8X4), scales=scales[:], in_=hw[e0][:].bitcast(BF16))
            for e in range(e0, e1):
                hq[e] = codes[:, (e - e0) * C : (e - e0 + 1) * C]
                hqs[e] = scales[:, (e - e0) * C : (e - e0 + 1) * C]

        def interleave(e, h, tag, first=nc.vector.tensor_copy):
            staged[e, h] = keep.tile([P, HALF * PACK], BF16, name="staged%d_%d" % (e, h), tag=tag, align_bytes=64)
            for m, copy in enumerate((first, nc.vector.tensor_copy)):
                copy(
                    staged[e, h][:, m * P * PACK : (m + 1) * P * PACK].rearrange("p (c i t) -> p c t i", i=4, t=PACK),
                    raw[e, h][:, :, m * P : (m + 1) * P].rearrange("p t (c i) -> p c t i", i=4),
                )

        def quantize_wb(e, h, tag=None):
            codes = keep.tile([P, HALF], U32, name="codes%d_%d" % (e, h), tag="codes%d_%d" % (e, h), align_bytes=64)
            scales = keep.tile([P, HALF], U8, name="scales%d_%d" % (e, h), tag=tag or "scales%d_%d" % (e, h), align_bytes=64)
            nc.vector.quantize_mx(out=codes[:].bitcast(FP8X4), scales=scales[:], in_=staged[e, h][:])
            for m in range(2):
                wbq[e, 2 * h + m] = codes[:, m * P : (m + 1) * P]
                wbqs[e, 2 * h + m] = scales[:, m * P : (m + 1) * P]

        def products(e, blocks, bank):
            acc = psum.tile([P, len(blocks), C], F32, name="acc%d_%d" % (e, blocks[0]), tag="bank%d" % bank)
            for m, b in enumerate(blocks):
                nc.tensor.matmul_mx(
                    out=acc[:, m, :], lhsT=w_sb[e][:, 2 * b * P : 2 * (b + 1) * P].bitcast(FP4X4),
                    lhsT_scale=ws_sb[e][:, b * P : (b + 1) * P], rhs=xg[e], rhs_scale=xgs[e],
                    start=(m == 0), stop=False,
                )
            for m, b in enumerate(blocks):
                nc.tensor.matmul_mx(
                    out=acc[:, m, :], lhsT=wbq[e, b].bitcast(FP8X4), lhsT_scale=wbqs[e, b],
                    rhs=hq[e].bitcast(FP8X4), rhs_scale=hqs[e], start=False, stop=(m == len(blocks) - 1),
                )
            return acc[:]

        def leave(e, acc, home):
            blocks = range(acc.shape[1])
            g = gates[:, e * C : (e + 1) * C].unsqueeze(1).to_broadcast([P, len(blocks), C])
            nc.vector.tensor_tensor(home, acc, g, MULT)

        def window(b, e0, e1):
            return windows[b][:].indirect(offsets[:, e0 * LIST_COLS : e1 * LIST_COLS])

        def store(b):
            nc.sync.dma_start(out[b * P : (b + 1) * P, :], windows[b][:])

        spread = psum.tile([P, PACK, P], F32, name="spread", tag="bank7")
        for j in range(PACK):
            nc.tensor.transpose(spread[:, j, :], gate_col[:, j : j + 1].to_broadcast([P, P]), ident[:])
        gates = keep.tile([P, E * C], F32, name="gates")
        nc.scalar.copy(gates[:].rearrange("p (n j) -> p n j", j=PACK), spread[:].rearrange("p j n -> p n j"))

        gather(0, 1)
        first_hidden(0)
        gather(1, 2)
        hidden(1, [3])
        gather(2, 4)
        interleave(0, 0, "first")
        quantize_wb(0, 0)
        quantize_h(0, 1, "first")
        turn(1, 2, 4)
        interleave(0, 1, "second")
        hidden(2, [1])
        hidden(3, [2])
        y0 = keep.tile([P, 4, C], F32, name="y0")
        for b in range(2):
            leave(0, products(0, [b], (7, 5)[b]), y0[:, b : b + 1, :])
        nc.scalar.activation(window(0, 0, 1), y0[:, 0, :], COPY)
        quantize_wb(0, 1, "h0")
        quantize_h(1, 2, "second")
        leave(0, products(0, [2, 3], 6), y0[:, 2:4, :])
        turn(2, 4, 7)
        nc.vector.tensor_copy(window(1, 0, 1), y0[:, 1, :])
        for b in (3, 2):
            nc.scalar.activation(window(b, 0, 1), y0[:, b, :], COPY)
        units = [(0, 0), (0, 1), (1, 0), (1, 1), (2, 0), (3, 0), (2, 1), (3, 1)]
        banks = (None, None, 1, 3, 4, 1, 4, 3)
        for u in (2, 3):
            interleave(*units[u], "codes%d_%d" % units[u - 2])
            quantize_wb(*units[u])
        quantize_h(2, 4, "codes0_0")
        homes = {
            2: keep.tile([P, 2, C], F32, name="y2", align_bytes=64)[:],
            3: raw[3, 0][:, 0:2, :C],
            6: raw[3, 1][:, 0:2, :C],
            7: raw[3, 1][:, 0:2, C:],
        }

        def finish(u, acc):
            e, h = units[u]
            leave(e, acc, homes[u])
            for m in (0,) if h == 1 else (1, 0):
                nc.scalar.activation(window(2 * h + m, e, e + 1), homes[u][:, m, :], COPY)

        def multiply(u):
            e, h = units[u]
            return products(e, [2 * h, 2 * h + 1], banks[u])

        acc = multiply(2)
        interleave(*units[4], "codes1_0", nc.scalar.copy)
        finish(2, acc)
        quantize_wb(*units[4])
        acc3 = multiply(3)
        interleave(*units[5], "codes1_1")
        leave(1, acc3[:, 0:1, :], homes[3][:, 0:1, :])
        nc.scalar.activation(window(2, 1, 2), homes[3][:, 0, :], COPY)
        quantize_wb(*units[5])
        homes[4] = raw[3, 0][:, 2:4, :C]
        finish(4, multiply(4))
        interleave(*units[6], "codes2_0")
        late = raw[2, 1][:, 2:3, :C]
        leave(1, acc3[:, 1:2, :], late)
        homes[5] = raw[2, 1][:, 0:2, :C]
        finish(5, multiply(5))
        quantize_wb(*units[6])
        nc.vector.tensor_copy(window(3, 1, 2), late[:, 0, :])
        interleave(*units[7], "codes3_0")
        quantize_wb(*units[7])
        store(1)
        store(0)
        finish(6, multiply(6))
        nc.vector.tensor_copy(window(3, 2, 3), homes[6][:, 1, :])
        finish(7, multiply(7))
        nc.vector.tensor_copy(window(3, 3, 4), homes[7][:, 1, :])
        store(3)
        store(2)
